import numpy as np, ml_dtypes
CORES = [9,25,41,57]
N = 4
import mx_ref
BF = ml_dtypes.bfloat16
def gentries(a):
    return np.ascontiguousarray(a.reshape(8, 16, -1).transpose(0, 2, 1)).reshape(8, -1)
def gtable(e):
    e = np.asarray(e); return np.ascontiguousarray(e.reshape(8, -1, 16).transpose(0, 2, 1)).reshape(128, -1).astype(np.int32)
def gcols(t, e):
    v = np.concatenate([t.reshape(8, 16, -1, 4), np.zeros((8, 16, 1, 4), BF)], axis=2)
    return np.ascontiguousarray(np.stack([v[g][:, e[g]] for g in range(8)])).reshape(128, -1)
def gpick(z, e):
    return np.concatenate([z[16 * g:16 * g + 16][:, e[g]] for g in range(8)])
def tile(rs):
    return np.stack(rs, axis=2).reshape(128, -1).astype(BF)
def pick(q, e):
    c = np.concatenate([q[0].reshape(128, -1, 4), np.zeros((128, 1, 4), np.uint8)], axis=1); s = np.concatenate([q[1], np.ones((16, 1), np.uint8)], axis=1)
    return (np.ascontiguousarray(c[:, e].reshape(128, -1)), np.ascontiguousarray(s[:, e]))
def join(*qs):
    return (np.concatenate([q[0] for q in qs], axis=1), np.concatenate([q[1] for q in qs], axis=1))
def put(q, e, v):
    c, s = q[0].reshape(128, -1, 4).copy(), q[1].copy(); c[:, e] = v[0].reshape(128, -1, 4); s[:, e] = v[1]
    return (c.reshape(128, -1), s)
def pk(c, s):
    return (np.ascontiguousarray(c), mx_ref.live(s))
def emit(q):
    return q[0], q[1]
def packed(v, rng):
    q = [mx_ref.quantize(np.ascontiguousarray(v[r])) for r in range(N)]
    return np.stack([a for a, b in q]), np.stack([mx_ref.plane(b, rng) for a, b in q])
def values_of_codes():
    e, c = np.zeros((128, 128, 4), np.float32), np.zeros((128, 2, 4), np.uint8)
    e[np.arange(128), np.arange(128), 0] = 1
    c[:127, :, 0] = np.arange(256).reshape(2, 128).T[:127]
    return mx_ref.matmul(mx_ref.quantize(e.reshape(128, 512).astype(BF)), (c.reshape(128, 8), np.full((16, 2), 127, np.uint8))).T.reshape(-1).astype(np.float64)
CODE_VALUE, SCALE_VALUE = values_of_codes(), 2.0 ** (np.arange(256) - 127.0)
def decode(q):
    return (CODE_VALUE[q[0]].reshape(16, 8, -1, 4) * SCALE_VALUE[q[1]][:, None, :, None] + 0.0).reshape(128, -1).astype(np.float32)
def f(rng, *shape):
    return mx_ref.flush((rng.standard_normal(shape, dtype=np.float32) * np.exp2(rng.integers(-2, 3, shape[:-1] + (1,)))).astype(BF))
def wide(rng, *shape, cols=0):
    v = rng.standard_normal(shape, dtype=np.float32) * np.exp2(rng.integers(-12, 13, shape)).astype(np.float32)
    if cols: v *= np.repeat(np.exp2(rng.integers(-cols, cols + 1, shape[:-2] + (1, shape[-1] // 4))) * (rng.random(shape[:-2] + (1, shape[-1] // 4)) > 0.0625), 4, axis=-1).astype(np.float32)
    return mx_ref.flush(v.astype(BF))
C = 448
STEP = [1, 2, 3]
def at(t, e):
    return np.take_along_axis(t, e, axis=1)
def ext(e):
    return np.concatenate([e, np.full((len(e), 1), C)], axis=1)
def numbers_of(rng):
    return {"x": np.array(f(rng, N, 128, 4 * C)), "u": np.array(f(rng, N, 128, 512)), "v": np.array(f(rng, N, 128, 512))}
def trees(rng, kind, o=None):
    n, kind = 8 * N, kind.reshape(-1)
    t = np.arange(n)
    if o is None: o = rng.permuted(np.tile(np.arange(C), (n, 1)), axis=1)
    free = np.tile(np.arange(C + 1), (n, 1))
    e = np.full((3, n, C), C)
    for i in range(1, C):
        k = rng.integers(0, i + 1, n)
        side = np.where(kind == 1, rng.integers(0, 2, n), kind - 3)
        slot = np.where(kind == 0, free[t, k], np.where(kind == 2, i - 1, 2 * i - 2 + side))
        free[t, k] = 2 * i
        free[:, i + 1] = 2 * i + 1
        a = o[t, slot // 2]
        e[0, t, o[:, i]] = a
        e[1 + slot % 2, t, a] = o[:, i]
    return e.reshape(3, N, 8, C)
def depths(p):
    h = ext(p.reshape(8 * N, C))
    d = (h < C).astype(np.int64)
    for k in range(9):
        d = d + at(d, h)
        h = at(h, h)
    return d[:, :C].reshape(N, 8, C)
def stored(e):
    return {k: np.stack([gtable(e[i, r]) for r in range(N)]) for i, k in enumerate(("up", "lf", "rt"))}
def lists(rng):
    return stored(trees(rng, np.zeros((N, 8), np.int64)))
def mixed(rng):
    return np.stack([rng.permutation([0, 0, 0, 1, 1, 2, 3, 4]) for r in range(N)])
def layers(rng, still=[]):
    w = np.array(f(rng, N, 128, 2048)).reshape(N, 8, 16, 4, 8, 16, 4)
    for i in still:
        w[:, :, i] = 0
        w[:, :, :, :, :, i] = 0
    return w
def weights(rng, w):
    c, p = packed(np.ascontiguousarray(w).reshape(N, 128, 2048), rng)
    return {"wc": c, "ws": p}
def setup_inputs(rng):
    return {**numbers_of(rng), **lists(rng), **weights(rng, layers(rng))}
def setup_inputs_ties(rng):
    d = numbers_of(rng)
    o = rng.permutation(N) % 4
    kind = mixed(rng)
    kind[o == 3] = 1
    e = trees(rng, kind)
    h = depths(e[0])
    k = rng.integers(0, 4, (N, 8, C))
    k[o == 0] = 5
    k[o == 1] = h[o == 1]
    k[o == 3] = h[o == 3] % 3 == 1
    x = d["x"].reshape(N, 8, 16, C, 4)
    x[:, :, :3] = 0
    u = d["u"].reshape(N, 128, 128, 4)
    u[:, :, ::16] = 0
    for i in range(3):
        x[:, :, i, :, 0] = (k // 8 ** i % 8).astype(np.float32).astype(BF)
        for c in range(0, 128, 16): u[:, c + i, c, 0] = 8.0 ** i
    return {"x": x.reshape(N, 128, 4 * C), "u": u.reshape(N, 128, 512), "v": d["v"], **stored(e), **weights(rng, layers(rng, [0, 1, 2]))}
def setup_inputs_near(rng):
    d = numbers_of(rng)
    x = d["x"].astype(np.float32).reshape(N, 8, 16, C, 4)
    x[:, :, 0] = 0
    x[:, :, 8:] = 0
    u = d["u"].reshape(N, 128, 128, 4)
    u[:, :, ::16] = 0
    o = (np.arange(N) + rng.integers(4)) % 4
    for r in range(N):
        c = np.where(rng.permutation(8)[:, None] < 4, rng.choice([-1.0, 1.0], (8, 1)), rng.choice([-1.0, 1.0], (8, C)))
        s = rng.integers(0, 16, (8, C))
        digits = ((s[:, :, None] >> np.arange(4)) & 1) * np.exp2(np.arange(4) - 23.0)
        if o[r] < 2:
            x[r, :, 0, :, 0] = c
            x[r, :, 8] = digits
            x[r, :, 11, :, 0] = c * 2.0 ** -10
        elif o[r] == 2: x[r, :, 8] = digits * rng.choice([-1.0, 1.0], (8, C, 1))
        else:
            a = rng.choice([-1.0, 1.0], (8, 1)) * 2.0 ** -30
            x[r, :, 8, :, 0] = np.where(s < 8, 1.25, 0.0) * a
            x[r, :, 9, :, 0] = np.where(s < 8, 0.0, 1.125) * a
            for g in rng.permutation(8)[:4]:
                e = rng.choice([-1.0, 1.0], C) * 2.0 ** -30
                x[r, g, 8, :, 0] = 1.25 * e
                x[r, g, 9, :, 0] = -1.125 * e
        if o[r] > 1: x[r, :, 12, :, 0] = rng.choice([1.0, 1.5], (8, C)) * 2.0 ** -30
        place = [0, C - 1, int(rng.integers(C)), int(rng.integers(C))]
        for g, j in zip(rng.permutation(8)[:4], place): x[r, g, 0, j, 0] = 2.0 ** 29 * rng.choice([-1.0, 1.0])
        k = 1.0 if o[r] == 0 else 2.0 ** -30
        for h in range(0, 128, 16):
            u[r, h, h, 0] = k if o[r] < 2 else 1.0
            if o[r] < 2: u[r, h + 11, h, 0] = k
            if o[r] < 3: u[r, h + 8, h] = k
            else:
                u[r, h + 8, h, 0] = k
                u[r, h + 9, h, 0] = 1.125 * k
                u[r, h + 10, h, 0] = k
    w = layers(rng, [0, 8, 9, 10, 11, 12, 13, 14, 15])
    for g in range(8): w[:, g, 12, 0, g, 10, 0] = 2.0 ** -8
    return {"x": x.reshape(N, 128, 4 * C).astype(BF), "u": u.reshape(N, 128, 512), "v": d["v"], **stored(trees(rng, mixed(rng))), **weights(rng, w)}
def setup_inputs_odd(rng):
    d = numbers_of(rng)
    o = rng.permutation(N) % 2
    x = (1.0 + (2 * rng.integers(0, 64, (N, 16, 8, C, 4)) + 1) * 2.0 ** -7) * np.exp2(-rng.integers(0, 7, (N, 16, 8, C, 4)).astype(np.float64)) * rng.choice([-1.0, 1.0], (N, 16, 8, C, 4))
    x[:, :, 0, :, 0] = rng.choice([1.96875, 1.875], (N, 16, C)) * 2.0 ** 8 * rng.choice([-1.0, 1.0], (N, 16, 1))
    u = d["u"].reshape(N, 16, 8, 128, 4)
    u[:, :, 0, ::16] = 0
    for r in range(N):
        if o[r]: continue
        for g, i in enumerate(rng.permutation(8) % 2):
            x[r, 2 * g, 1, :, 0] = (8 + rng.integers(0, 2, C)) * 2.0 ** (i - 8.0)
            u[r, :, :, 16 * g] = 0
            u[r, 2 * g, 1, 16 * g, 0] = 1.0
    return {"x": x.astype(np.float32).reshape(N, 128, 4 * C).astype(BF), "u": u.reshape(N, 128, 512), "v": d["v"], **lists(rng), **weights(rng, layers(rng, [0, 8]))}
def setup_inputs_ends(rng):
    d = numbers_of(rng)
    o = (np.arange(N) + rng.integers(4)) % 4
    big = (o < 2)[:, None, None, None]
    def sized(*n):
        return np.where(big, (0.955 + 0.02 * rng.random((N,) + n)) * 2.0 ** 30, (1.0 + 0.125 * rng.integers(0, 8, (N,) + n)) * 2.0 ** -30)
    s = rng.choice([-1.0, 1.0], (N, 128, C, 4))
    s[o == 1] = rng.choice([-1.0, 1.0], (N, 1, C, 1))[o == 1]
    s[o == 3] = rng.choice([-1.0, 1.0], (N, 128, 1, 4))[o == 3]
    s[o % 2 == 0] = -1
    x = s * sized(128, C, 4)
    h = np.stack([rng.permutation(8) for r in range(N)])
    u = d["u"].reshape(N, 128, 128, 4)
    u[:, :, ::16] = (np.where(h < 2, 0.0, h % 2 * 2.0 - 1.0)[:, None, :, None] * sized(128, 8, 4)).astype(np.float32).astype(BF)
    v = rng.choice([-1.0, 1.0], (N, 128, 128, 4)) * sized(128, 128, 4)
    w = np.zeros((N, 128, 4, 128, 4), np.float32)
    i = np.arange(128)
    for b in range(4): w[:, i, b, i, b] = np.array([-0.125, -0.125, -2.0 ** -8, 2.0 ** 4])[o][:, None]
    kind = np.stack([rng.permutation([0, 1, 2, 2, 3, 3, 4, 4]) for r in range(N)])
    fall = np.stack([rng.permutation(8) % 2 for r in range(N)]).reshape(-1, 1)
    k = np.tile(np.arange(C), (8 * N, 1))
    return {"x": x.astype(np.float32).reshape(N, 128, 4 * C).astype(BF), "u": u.reshape(N, 128, 512), "v": v.astype(np.float32).reshape(N, 128, 512).astype(BF), **stored(trees(rng, kind, np.where(fall == 0, k, C - 1 - k))), **weights(rng, w.astype(BF))}
def setup_inputs_spread(rng):
    d = setup_inputs(rng)
    d["x"] = wide(rng, N, 128, 4 * C, cols=6)
    return d
def check_inputs(d):
    b = []
    for k in ("x", "u", "v"):
        a = np.abs(d[k].astype(np.float32))
        if not (np.isfinite(a).all() and ((a == 0) | (a >= 2.0 ** -30) & (a <= 2.0 ** 30)).all()): b.append("a value of " + k)
    bad = [k for k in ("up", "lf", "rt") if not ((d[k] >= 0) & (d[k] <= C)).all()]
    b += ["an entry of " + k for k in bad]
    none, least, most = [emit(mx_ref.quantize(np.full((128, 16), k, np.float32).astype(BF)))[1][0, 0] for k in (0.0, 2.0 ** -8, 2.0 ** 8)]
    own = np.arange(C + 1)
    for r in range(N):
        if ((d["wc"][r] == 0x7F) | (d["wc"][r] == 0xFF)).any(): b.append("wc: a code that is no number")
        s = mx_ref.live(d["ws"][r])
        if ((s != none) & ((s < least) | (s > most))).any(): b.append("ws: a scale out of range")
        if bad: continue
        p, l, e = [ext(gentries(d[k][r])) for k in ("up", "lf", "rt")]
        ok = (np.sum(p[:, :C] == C, axis=1) == 1).all() and (np.sum(l < C, axis=1) + np.sum(e < C, axis=1) == C - 1).all()
        ok = ok and ((l == C) | (l != e)).all() and all(((k == C) | (at(p, k) == own)).all() for k in (l, e))
        for k in range(9): p = at(p, p)
        if not (ok and (p == C).all()): b.append("up, lf, rt: not a tree")
    return b
def rotated(s, p, l, r):
    own = np.tile(np.arange(C + 1), (8, 1))
    w = np.concatenate([s, np.zeros((8, 1), np.float32)], axis=1)
    gain = np.where(p < C, np.maximum(w - at(w, p), np.float32(0)), np.float32(0))
    def better(a, b):
        i, j = at(gain, a), at(gain, b)
        return np.where((i > j) | (i == j) & (a < b), a, b)
    child = better(l, r)
    best = better(better(own, child), better(at(child, l), at(child, r)))
    z = at(p, p)
    g, v = np.nonzero((gain > 0) & (best == own) & (at(best, p) == own) & ((z == C) | (at(best, z) == own)))
    y, z = p[g, v], z[g, v]
    left, high = l[g, y] == v, l[g, z] == y
    c = np.where(left, r[g, v], l[g, v])
    a, b, e = p.copy(), l.copy(), r.copy()
    a[g, c], a[g, y], a[g, v] = y, v, z
    b[g, y], e[g, y] = np.where(left, c, l[g, y]), np.where(left, r[g, y], c)
    b[g, v], e[g, v] = np.where(left, l[g, v], y), np.where(left, y, r[g, v])
    b[g, z], e[g, z] = np.where(high, v, l[g, z]), np.where(high, r[g, z], v)
    for k in (a, b, e): k[:, C] = C
    return a, b, e
def reference(x, u, v, up, lf, rt, wc, ws):
    qu = [mx_ref.quantize(u[r]) for r in range(N)]
    lay = [pk(wc[r], ws[r]) for r in range(N)]
    link = [[ext(gentries(k[r])) for k in (up, lf, rt)] for r in range(N)]
    now = [x[r] for r in range(N)]
    for step in STEP:
        t, par, z = [], [], []
        for r in range(N):
            q = mx_ref.quantize(now[r])
            link[r] = rotated(mx_ref.matmul(qu[r], q)[::16] + np.float32(0.0), *link[r])
            p = link[r][0][:, :C]
            a = np.where(p == C, np.arange(C), p)
            t.append(decode(q))
            par.append(a)
            m = t[r].astype(BF)
            z.append(mx_ref.quantize(((gcols(m, a).astype(np.float32) + gcols(m, at(a, a)).astype(np.float32)) * np.float32(0.5)).astype(BF)))
        for r in range(N):
            now[r] = tile([gpick(mx_ref.matmul(pick(lay[r], np.arange(128 * b, 128 * b + 128)), z[(r - step) % N]) * np.float32(0.03125), par[r]) + t[r][:, b::4] for b in range(4)])
    y, tr = np.zeros((N, 128, C), np.float32), np.zeros((N, 8, 3 * C), np.float32)
    oc, osc = np.zeros((N, 128, 4 * C), np.uint8), np.zeros((N, 16, C), np.uint8)
    for r in range(N):
        q = mx_ref.quantize(now[r])
        y[r] = mx_ref.matmul(mx_ref.quantize(v[r]), q)
        tr[r] = np.concatenate([k[:, :C] for k in link[r]], axis=1)
        oc[r], osc[r] = emit(q)
    return {"y": y, "tr": tr, "oc": oc, "osc": osc}

@@ -1,0 +1,523 @@
+from concourse.mybir import dt, AluOpType, ActivationFunctionType
+
+N = 4
+C = 448
+H = 224
+STEP = [1, 2, 3]
+BIGV = 3.0e29
+
+F32, BF, U16, I32, CODE, PLANE = "float32", "bfloat16", "uint16", "int32", "float8_e4m3fn_x4", "uint8"
+SCRATCH = {"ps": ("psum", [128, 4096], F32)}
+
+
+def _sbuf(names, n, dtype):
+    for k in names.split():
+        SCRATCH[k] = ("sbuf", [128, n], dtype)
+
+
+_sbuf("xt xn zt", 4 * C, BF)
+_sbuf("ut vt ones et0 et1 et2 et3", 512, BF)
+_sbuf("uq vq", 128, CODE)
+_sbuf("us vs", 128, PLANE)
+_sbuf("wq eq", 512, CODE)
+_sbuf("wp es", 512, PLANE)
+_sbuf("zq q0 q1 q2 q3 aq0 aq1 aq2", C, CODE)
+_sbuf("zs qs0 qs1 qs2 qs3 as0 as1 as2", C, PLANE)
+_sbuf("pidx", 2, I32)
+_sbuf("ti", 16, I32)
+_sbuf("c224", 8, F32)
+_sbuf("offm0 offm1", 2, U16)
+_sbuf("upi lfi rti", 28, I32)
+_sbuf("al0 al1 al2", 28, U16)
+_sbuf("lup la0 la1 la2 la3 ll0 ll1 lr0 lr1", 32, U16)
+_sbuf("iot prow rrow ra qrow rrep", 464, BF)
+_sbuf("srow urow", 456, F32)
+_sbuf("nT lrow raa pT lT rT raT raaT pp ppT qa qaa qaaa ql qr qaT qaaT qaaaT qlT qrT repl repr_ replT reprT rp2", C, BF)
+_sbuf("sa sl sr sT saT slT srT ulT urT trf yt rr0 rr1 rr2 rr3", C, F32)
+_sbuf("wu", C, F32)
+_sbuf("wc_ wr wp2", C, BF)
+_sbuf("ba0 ba1 bl0 bl1", C + 480, BF)
+_sbuf("rw rw2", 512, BF)
+_sbuf("m3 v3", 84, F32)
+_sbuf("cb", 28 * 80, F32)
+_sbuf("fo0 fo1 fo2 fo3 fp0 fp1 fp2 fp3", C, BF)
+_sbuf("fq kb", 4 * C, BF)
+
+SEMAPHORES = (["cv", "cs", "ct", "cg", "sent"] + ["ld_" + k for k in "x u v up lf rt wc ws".split()]
+              + ["st_" + k for k in "y oc osc tr".split()] + ["cf%d" % k for k in range(4)] + ["arq%d" % k for k in range(3)] + ["arl%d" % k for k in range(3)])
+
+
+def rank_program(g, core, T, topo):
+    rank = T.rank_of(core)
+    if rank is None:
+        return
+    A = AluOpType
+    ACT = ActivationFunctionType
+    V, S = g.vector, g.scalar
+    queue = {"v": V, "s": S, "t": g.tensor, "g": g, "y": g.sync}
+
+    count = {}
+    seen = {k: {} for k in queue}
+    facts = {}
+    writer, readers = {}, {}
+
+    def wait(q, sem, val):
+        s = seen[q]
+        if s.get(sem, 0) >= val:
+            return
+        queue[q].wait_ge(T.sem[sem], val)
+        s[sem] = val
+        for k, n in facts.get((sem, val), {}).items():
+            if s.get(k, 0) < n:
+                s[k] = n
+
+    def prepare(q, reads, writes):
+        need = {}
+        for k in reads + writes:
+            if k in writer:
+                w, n, wq = writer[k]
+                need[w] = max(need.get(w, 0), n)
+        for k in writes:
+            for w, n, rq in readers.get(k, []):
+                if rq != q or w[0] != "c":
+                    need[w] = max(need.get(w, 0), n)
+        own = "c" + q
+        for w in sorted(need, key=lambda w: (w == own, w)):
+            wait(q, w, need[w])
+
+    def note(q, sem, val, reads, writes):
+        facts[(sem, val)] = dict(seen[q])
+        for k in writes:
+            writer[k] = (sem, val, q)
+            readers[k] = []
+        for k in reads:
+            readers.setdefault(k, []).append((sem, val, q))
+
+    def op(q, fn, reads, writes):
+        prepare(q, reads, writes)
+        sem = "c" + q
+        count[sem] = count.get(sem, 0) + 1
+        fn().then_inc(T.sem[sem], 1)
+        note(q, sem, count[sem], reads, writes)
+
+    def dma(q, sem, out, in_, reads, writes):
+        prepare(q, reads, writes)
+        count[sem] = count.get(sem, 0) + 16
+        queue[q].dma_start(out, in_).then_inc(T.sem[sem], 16)
+        note(q, sem, count[sem], reads, writes)
+
+    def send(dst, rsem, out, in_, reads):
+        prepare("g", reads, [])
+        rid, pid, se = topo.addr(dst)
+        g.remote_dma(out, in_, T.sem[rsem], T.sem["sent"], pid, rid, topo.mask(core, dst))
+        count["sent"] = count.get("sent", 0) + len(topo.engines(core, dst))
+
+    def ps(b, n=C):
+        return T.ps[:, 512 * b:512 * b + n]
+
+    slots = {}
+
+    def slot(name):
+        i = slots.setdefault(name, len(slots))
+        return T.cb[:, 28 * i:28 * i + 28], "cb." + name
+
+    def plane(buf, lane):
+        return T[buf][:, lane:C:16], buf
+
+    def sub(buf, lane):
+        return T[buf][:, lane:C:16], "%s.%d" % (buf, lane)
+
+    def tt(out, a, b, o):
+        op("v", lambda: V.tensor_tensor(out[0], a[0], b[0], o), [a[1], b[1]], [out[1]])
+        return out
+
+    def ts(out, a, s1, o1, s2=None, o2=None):
+        if o2 is None:
+            op("v", lambda: V.tensor_scalar(out[0], a[0], s1, None, o1), [a[1]], [out[1]])
+        else:
+            op("v", lambda: V.tensor_scalar(out[0], a[0], s1, s2, o1, o2), [a[1]], [out[1]])
+        return out
+
+    def turn(out, ok, in_, ik):
+        op("v", lambda: V.transpose(out, in_), ik, ok)
+
+    def turned(out, in_):
+        turn(T[out][:], [out], T[in_][:, 0:C], [in_])
+
+    def gather(q, out, win, wk, off, fk):
+        if q == "s":
+            op("s", lambda: S.activation(out[0], win.indirect(off), ACT.Copy), wk + [fk], [out[1]])
+        else:
+            op("v", lambda: V.tensor_copy(out[0], win.indirect(off)), wk + [fk], [out[1]])
+
+    def row(buf):
+        return T[buf][:], buf
+
+    def memset(ap, val, keys):
+        op("v", lambda: V.memset(ap, val), [], keys)
+
+    def mm(bank, l, ls, r, rs, keys, n=C):
+        op("t", lambda: g.tensor.matmul_mx(ps(bank, n), l, ls, r, rs, True, True), keys, ["ps%d" % bank])
+
+    def quantize(out, os, in_, reads, writes):
+        op("v", lambda: V.quantize_mx(out, os, in_), reads, writes)
+
+    def blk(buf, b):
+        return T[buf][:, 128 * b:128 * b + 128]
+
+    todo = []
+
+    def fill(n=1):
+        for _ in range(n):
+            if todo:
+                todo.pop(0)()
+
+    dma("y", "ld_up", T.upi[:], T.up[:], [], ["upi"])
+    dma("s", "ld_rt", T.rti[:], T.rt[:], [], ["rti"])
+    dma("s", "ld_lf", T.lfi[:], T.lf[:], [], ["lfi"])
+    dma("y", "ld_x", T.xt[:], T.x[:], [], ["xt"])
+    dma("y", "ld_u", T.ut[:], T.u[:], [], ["ut"])
+    dma("y", "ld_wc", T.wq[:, 0:512].bitcast(dt.uint8), T.wc[:], [], ["wq"])
+    dma("y", "ld_ws", T.wp[:, 0:512], T.ws[:], [], ["wp"])
+    dma("y", "ld_v", T.vt[:], T.v[:], [], ["vt"])
+
+    op("g", lambda: g.iota(T.pidx[:], [[0, 2]], 0, 1), [], ["pidx"])
+    memset(T.ones[:], 1.0, ["ones"])
+    op("g", lambda: g.affine_select(T.et0[:], T.ones[:], [[-1, 512]], A.is_equal, 0.0, 0, 4), ["ones"], ["et0"])
+    op("g", lambda: g.iota(T.iot[:], [[1, 464]], -224, 0, allow_small_or_imprecise_dtypes=True), [], ["iot"])
+    for b in range(1, 4):
+        memset(T["et%d" % b][:, 0:b], 0.0, ["et%d.0" % b])
+        op("s", lambda: S.activation(T["et%d" % b][:, b:512], T.et0[:, 0:512 - b], ACT.Copy), ["et0"], ["et%d" % b])
+    memset(T.ba0[:, 0:C], 0.0, ["ba0.0", "ba0.i"])
+    memset(T.rw[:, 0:32], 0.0, ["rw.p0"])
+    memset(T.rw[:, 480:512], 0.0, ["rw.p1"])
+    for k in ("prow", "rrow", "ra"):
+        memset(T[k][:, C:464], 224.0, [k + ".n"])
+    memset(T.srow[:, C:456], -BIGV, ["srow.n"])
+    memset(T.urow[:, C:456], BIGV, ["urow.n"])
+    memset(T.qrow[:, C:464], 600.0, ["qrow.n"])
+    memset(T.c224[:], 224.0, ["c224"])
+
+    def tiv(i):
+        return T.ti[:, i:i + 1], "ti%d" % i
+    pd = (T.pidx[:, 0:1], "pidx")
+    ts(tiv(0), pd, 1, A.logical_shift_right, 7, A.bitwise_and)
+    ts(tiv(1), pd, 1, A.bitwise_and)
+    ts(tiv(2), pd, 4, A.logical_shift_right, 1, A.bitwise_and)
+    ts(tiv(4), tiv(0), 32, A.mult)
+    tt(tiv(3), tiv(1), tiv(2), A.mult)
+    ts(tiv(5), tiv(1), 480, A.mult)
+    ts(tiv(6), tiv(2), 464, A.mult)
+    ts(tiv(7), tiv(3), -928, A.mult)
+    tt(tiv(8), tiv(4), tiv(5), A.add)
+    tt(tiv(9), tiv(6), tiv(7), A.add)
+    tt(tiv(10), tiv(8), tiv(9), A.add)
+    for h in range(2):
+        ts((T.offm0[:, h:h + 1], "offm0"), tiv(10), 256 * h, A.add, 927, A.min)
+
+    def turned_back(big, rw, lanes, between=None):
+        turn(T[rw][:, 32:480], [rw], T[big][:, 0:C], ["%s.%s" % (big, k) for k in lanes] + [big + ".i"])
+        if between:
+            between()
+        turn(T[big][:, C:928], [big + ".s"], T[rw][:, 16:496], [rw, rw + ".p0", rw + ".p1"])
+
+    def make_list(out, big, lane):
+        op("v", lambda: V.tensor_scalar(T[out][:], T[big][:, 0:928].indirect(T["offm%d" % lane][:]), 224.0, None, A.add),
+           ["%s.%d" % (big, lane), big + ".i", big + ".s", "offm%d" % lane], [out])
+
+    nv = plane("nT", 0)
+    turned("nT", "iot")
+    op("v", lambda: V.tensor_copy(T.lup[:, 0:28], T.upi[:]), ["upi"], ["lup"])
+    lup = T.lup[:, 0:28]
+    gather("v", (T.prow[:, 0:C], "prow"), T.iot[:], ["iot"], lup, "lup")
+    op("v", lambda: V.tensor_copy(T.lr0[:, 0:28], T.rti[:]), ["rti"], ["lr0"])
+    op("v", lambda: V.tensor_copy(T.ll0[:, 0:28], T.lfi[:]), ["lfi"], ["ll0"])
+    gather("s", (T.rrow[:, 0:C], "rrow"), T.iot[:], ["iot"], T.lr0[:, 0:28], "lr0")
+    gather("s", row("lrow"), T.iot[:], ["iot"], T.ll0[:, 0:28], "ll0")
+    gather("s", (T.ra[:, 0:C], "ra"), T.rrow[:], ["rrow", "rrow.n"], lup, "lup")
+    gather("s", row("raa"), T.ra[:], ["ra", "ra.n"], lup, "lup")
+    gather("s", row("pp"), T.prow[:], ["prow", "prow.n"], lup, "lup")
+    turned("pT", "prow")
+    pT = plane("pT", 0)
+    e = ts(slot("i0"), pT, 224.0, A.is_equal)
+    f_ = tt(slot("i1"), nv, pT, A.subtract)
+    f_ = tt(slot("i2"), e, f_, A.mult)
+    tt(sub("ba0", 0), pT, f_, A.add)
+    for b in range(4):
+        quantize(blk("eq", b), blk("es", b), T["et%d" % b][:], ["et%d" % b] + (["et%d.0" % b] if b else []), ["eq%d" % b])
+        if b == 0:
+            turned_back("ba0", "rw", [0])
+        if b == 1:
+            make_list("la0", "ba0", 0)
+    turned("rT", "rrow")
+    turned("lT", "lrow")
+    lv, rv = plane("lT", 0), plane("rT", 0)
+
+    def m3(i):
+        return T.m3[:, 28 * i:28 * i + 28], "m3.%d" % i
+
+    def v3(i):
+        return T.v3[:, 28 * i:28 * i + 28], "v3.%d" % i
+    ts(m3(0), nv, -256.0, A.add)
+    ts(m3(1), lv, -256.0, A.add)
+    ts(m3(2), rv, -256.0, A.add)
+    memset(T.wu[:], 0.0, ["wu.0", "wu.1", "wu.i"])
+    memset(T.wc_[:], 0.0, ["wc_.0", "wc_.i"])
+    quantize(T.q0[:], T.qs0[:], T.xt[:], ["xt"], ["q0"])
+    quantize(T.uq[:], T.us[:], T.ut[:], ["ut"], ["uq"])
+    for h in range(2):
+        ts((T.offm1[:, h:h + 1], "offm1"), tiv(10), 256 * h + 1, A.add, 927, A.min)
+    memset(T.ba1[:, 0:C], 0.0, ["ba1.0", "ba1.i"])
+
+    def late_constants():
+        memset(T.rrep[:, C:464], 224.0, ["rrep.n"])
+        memset(T.wr[:], 0.0, ["wr.0", "wr.i"])
+
+    def later_constants():
+        memset(T.wp2[:], 0.0, ["wp2.1", "wp2.2", "wp2.i"])
+        memset(T.rw2[:, 0:32], 0.0, ["rw2.p0"])
+        memset(T.rw2[:, 480:512], 0.0, ["rw2.p1"])
+        memset(T.bl0[:, 0:C], 0.0, ["bl0.0", "bl0.1", "bl0.i"])
+        memset(T.bl1[:, 0:C], 0.0, ["bl1.0", "bl1.1", "bl1.2", "bl1.i"])
+
+    def derive(k, pv, sv, lv, rv):
+        def add(f, *a):
+            todo.append(lambda: f(*a))
+        ppv, spv = plane("ppT", 1), plane("ppT", 2)
+        if k == 0:
+            ppv, spv = plane("ppT", 0), slot("sp0")
+            for n in ("raT raaT ppT").split():
+                add(turned, n, n[:-1])
+            add(tt, sv, plane("raT", 0), nv, A.is_equal)
+            add(tt, spv, plane("raaT", 0), pv, A.is_equal)
+            add(ts, slot("d0"), ppv, 224.0, A.is_equal)
+        else:
+            add(turned, "ppT", "pp")
+            add(tt, slot("d0"), ppv, pv, A.is_equal)
+        add(tt, slot("d1"), nv, ppv, A.subtract)
+        add(tt, slot("d2"), sv, spv, A.is_equal)
+        add(tt, slot("d3"), lv, rv, A.subtract)
+        add(tt, slot("d4"), slot("d0"), slot("d1"), A.mult)
+        add(ts, slot("d5"), slot("d2"), 2048.0, A.mult)
+        add(tt, slot("d6"), sv, slot("d3"), A.mult)
+        add(tt, slot("d7"), ppv, slot("d4"), A.add)
+        add(tt, slot("pin"), slot("d5"), pv, A.add)
+        add(tt, slot("d8"), rv, slot("d6"), A.add)
+        add(tt, slot("dz"), slot("d7"), pv, A.subtract)
+        add(tt, slot("cn"), slot("d8"), nv, A.subtract)
+        add(tt, slot("sd"), spv, sv, A.subtract)
+        add(ts, slot("s2"), sv, -2.0, A.mult, 1.0, A.add)
+
+    pv, sv = sub("ba0", 0), slot("side0")
+    for k in range(3):
+        par, nxt = k % 2, 1 - k % 2
+        last = k == 2
+        q, qs, qk = T["q%d" % k], T["qs%d" % k], "q%d" % k
+        dst = T.cores[(rank + STEP[k]) % N]
+        la, lak = T["la%d" % k][:, 0:28], "la%d" % k
+        ll, llk = T["ll%d" % par][:, 0:28], "ll%d" % par
+        lr, lrk = T["lr%d" % par][:, 0:28], "lr%d" % par
+        lak2 = "la%d" % (k + 1)
+        la2 = T[lak2][:, 0:28]
+        send(dst, "arq%d" % k, T["aq%d" % k][:, 0:C].bitcast(dt.uint8), q[:, 0:C].bitcast(dt.uint8), [qk])
+        send(dst, "arq%d" % k, T["as%d" % k][:, 0:C], qs[:, 0:C], [qk])
+        mm(0, T.uq[:], T.us[:], q[:, 0:H], qs[:, 0:H], ["uq", qk], H)
+        mm(7, T.uq[:], T.us[:], q[:, H:C], qs[:, H:C], ["uq", qk], H)
+        for b in range(4):
+            mm(1 + b, blk("eq", b), blk("es", b), q[:], qs[:], ["eq%d" % b, qk])
+        op("v", lambda: V.tensor_copy(T.srow[:, 0:H], ps(0, H)), ["ps0"], ["srow.a"])
+        op("s", lambda: S.activation(T.srow[:, H:C], ps(7, H), ACT.Copy), ["ps7"], ["srow.b"])
+        sk = ["srow.a", "srow.b", "srow.n"]
+        gather("s", row("sl"), T.srow[:, 0:456], sk, ll, llk)
+        gather("s", row("sr"), T.srow[:, 0:456], sk, lr, lrk)
+        if k:
+            turn(T.rp2[:], ["rp2"], T.wp2[:], ["wp2.1", "wp2.2", "wp2.i"])
+            gather("s", row("pp"), T.rp2[:], ["rp2"], la, lak)
+        for b in range(4):
+            op("s", lambda: S.activation(T["fo%d" % b][:], ps(1 + b), ACT.Copy), ["ps%d" % (1 + b)], ["fo%d" % b])
+        derive(k, pv, sv, lv, rv)
+        gather("v", row("sa"), T.srow[:, 0:456], sk, la, lak)
+        turn(T.sT[:], ["sT"], T.srow[:, 0:C], sk)
+        turned("saT", "sa")
+        s0, sav, slv, srv = plane("sT", 0), plane("saT", 0), plane("slT", 0), plane("srT", 0)
+        turned("slT", "sl")
+        tt(v3(0), sav, s0, A.subtract)
+        turned("srT", "sr")
+        tt(v3(1), s0, slv, A.subtract)
+        tt(v3(2), s0, srv, A.subtract)
+        tt(slot("m"), v3(0), v3(1), A.min)
+        ts(slot("v0c"), v3(0), -1.0e-30, A.min)
+        u0, u1 = sub("wu", 0), sub("wu", 1)
+        tt(u0, slot("m"), v3(2), A.min)
+        fill()
+        for i in range(3):
+            tt(slot("e%d" % i), v3(i), u0, A.is_equal)
+        for i in range(3):
+            tt(slot("t%d" % i), slot("e%d" % i), m3(i), A.mult)
+        tt(slot("t3"), slot("t0"), slot("t1"), A.min)
+        fill()
+        tt(u1, slot("t3"), slot("t2"), A.min)
+        fill()
+        turn(T.urow[:, 0:C], ["urow"], T.wu[:], ["wu.0", "wu.1", "wu.i"])
+        uk = ["urow", "urow.n"]
+        gather("s", row("sl"), T.urow[:, 0:456], uk, ll, llk)
+        fill()
+        gather("v", row("sr"), T.urow[:, 0:456], uk, lr, lrk)
+        if k == 0:
+            late_constants()
+        turned("ulT", "sl")
+        turned("urT", "sr")
+        tt(slot("m"), slot("v0c"), plane("ulT", 0), A.min)
+        fill()
+        m = tt(slot("mm"), slot("m"), plane("urT", 0), A.min)
+        fill()
+        tt(slot("e0"), v3(0), m, A.is_equal)
+        tt(slot("e1"), plane("ulT", 0), m, A.is_equal)
+        tt(slot("e2"), plane("urT", 0), m, A.is_equal)
+        tt(slot("t0"), slot("e0"), m3(0), A.mult)
+        tt(slot("t1"), slot("e1"), plane("ulT", 1), A.mult)
+        tt(slot("t2"), slot("e2"), plane("urT", 1), A.mult)
+        tt(slot("t3"), slot("t0"), slot("t1"), A.min)
+        fill()
+        tt(slot("t4"), slot("t2"), slot("t3"), A.min)
+        fill()
+        Q0 = ts(sub("wc_", 0), slot("t4"), 256.0, A.add)
+        fill()
+        turn(T.qrow[:, 0:C], ["qrow"], T.wc_[:], ["wc_.0", "wc_.i"])
+        gather("s", row("qa"), T.qrow[:, 0:C], ["qrow"], la, lak)
+        gather("s", row("qaa"), T.qa[:], ["qa"], la, lak)
+        fill()
+        gather("v", row("ql"), T.qrow[:], ["qrow", "qrow.n"], ll, llk)
+        gather("s", row("qr"), T.qrow[:], ["qrow", "qrow.n"], lr, lrk)
+        gather("s", row("qaaa"), T.qaa[:], ["qaa"], la, lak)
+        fill(len(todo))
+        turned("qaT", "qa")
+        turned("qlT", "ql")
+        Qa, Qaa, Qaaa, Ql, Qr = plane("qaT", 0), plane("qaaT", 0), plane("qaaaT", 0), plane("qlT", 0), plane("qrT", 0)
+        eA = tt(slot("eA"), Q0, Qa, A.is_equal)
+        xn = tt(slot("xn"), Qa, nv, A.is_equal)
+        xl = tt(slot("xl"), Qa, lv, A.is_equal)
+        xp = tt(slot("xp"), Qa, slot("pin"), A.is_equal)
+        xr = tt(slot("xr"), Qa, rv, A.is_equal)
+        eL = tt(slot("eL"), Ql, Qa, A.is_equal)
+        rn = tt(slot("rn"), xn, eA, A.mult)
+        yq = tt(slot("yq"), Qa, pv, A.subtract)
+        yl = tt(slot("yl"), xl, eL, A.mult)
+        turned("qaaT", "qaa")
+        xr = tt(slot("xra"), xr, eA, A.mult)
+        YL = tt(slot("YL"), yl, eA, A.mult)
+        eB = tt(slot("eB"), Qaa, Qa, A.is_equal)
+        rot = tt(slot("rot"), rn, eB, A.mult)
+        xb = tt(slot("xb"), xp, eB, A.mult)
+        turned("qrT", "qr")
+        rd = tt(slot("rd"), rot, slot("dz"), A.mult)
+        xbd = tt(slot("xbd"), xb, slot("dz"), A.mult)
+        eR = tt(slot("eR"), Qr, Qa, A.is_equal)
+        rd = tt(slot("rd2"), rd, pv, A.add)
+        YR = tt(slot("YR"), xr, eR, A.mult)
+        Y = tt(slot("Y"), YL, YR, A.add)
+        yd = tt(slot("yd"), Y, yq, A.mult)
+        base = tt(slot("base"), rd, yd, A.add)
+        turned("qaaaT", "qaaa")
+        eC = tt(slot("eC"), Qaaa, Qa, A.is_equal)
+        t = tt(slot("r0"), Qa, nv, A.subtract)
+        cd = tt(slot("cd"), xbd, eC, A.mult)
+        fr = tt(slot("r1"), rot, slot("cn"), A.mult)
+        pn = tt(sub("ba%d" % nxt, 0), base, cd, A.add)
+        t = tt(slot("r2"), Y, t, A.mult)
+        turned_back("ba%d" % nxt, "rw", [0], lambda: tt(slot("r3"), fr, nv, A.add))
+        tt(sub("wr", 0), slot("r3"), t, A.add)
+        make_list(lak2, "ba%d" % nxt, 0)
+        send(dst, "arl%d" % k, T["al%d" % k][:], la2, [lak2])
+        wait("t", "arq%d" % k, 2 * len(topo.engines(core, dst)))
+        fbank = [5, 6, 7, 0]
+        for b in range(4):
+            mm(fbank[b], blk("eq", b), blk("es", b), T["aq%d" % k][:], T["as%d" % k][:], ["eq%d" % b])
+        for b in range(4):
+            op("s", lambda: S.activation(T["fp%d" % b][:], ps(fbank[b]), ACT.Copy), ["ps%d" % fbank[b]], ["fp%d" % b])
+            dma("y", "cf%d" % b, T.fq[:, C * b:C * b + C], T["fp%d" % b][:], ["fp%d" % b], ["fq%d" % b])
+        isc = tt(slot("isc"), xb, eC, A.mult)
+        rs1 = tt(slot("rs1"), rot, sv, A.mult)
+        turn(T.rrep[:, 0:C], ["rrep"], T.wr[:], ["wr.0", "wr.i"])
+        rk = ["rrep", "rrep.n"]
+        gather("s", row("repl"), T.rrep[:], rk, ll, llk)
+        gather("s", row("repr_"), T.rrep[:], rk, lr, lrk)
+        rs0 = tt(slot("rs0"), rot, rs1, A.subtract)
+        if not last:
+            t1 = tt(slot("s3"), rot, slot("sd"), A.mult)
+            t2 = tt(slot("s4"), isc, slot("s2"), A.mult)
+            t3 = tt(slot("s5"), Y, sv, A.mult)
+            t1 = tt(slot("s6"), sv, t1, A.add)
+            t3 = tt(slot("s7"), YL, t3, A.subtract)
+            t1 = tt(slot("s8"), t1, t2, A.add)
+            sn = tt(slot("side%d" % nxt), t1, t3, A.add)
+        else:
+            quantize(T.vq[:], T.vs[:], T.vt[:], ["vt"], ["vq"])
+        if k == 0:
+            later_constants()
+        if not last:
+            ts(sub("wp2", 1), pn, 0.0, A.add)
+            ts(sub("wp2", 2), sn, 0.0, A.add)
+        turned("replT", "repl")
+        turned("reprT", "repr_")
+        Rl, Rr = plane("replT", 0), plane("reprT", 0)
+        lnew, rnew = sub("bl%d" % nxt, 0), sub("bl%d" % nxt, 1)
+        t1 = tt(slot("l0"), pv, Rl, A.subtract)
+        t2 = tt(slot("l1"), pv, Rr, A.subtract)
+        t1 = tt(slot("l2"), rs1, t1, A.mult)
+        t2 = tt(slot("l3"), rs0, t2, A.mult)
+        tt(lnew, Rl, t1, A.add)
+        tt(rnew, Rr, t2, A.add)
+        wait("v", "arl%d" % k, len(topo.engines(core, dst)))
+        wait("s", "arl%d" % k, len(topo.engines(core, dst)))
+        al = T["al%d" % k]
+        for b in range(4):
+            fp, fq, kb = T["fp%d" % b], T.fq[:, C * b:C * b + C], T.kb[:, C * b:C * b + C]
+            op("v", lambda: V.tensor_tensor(kb, fp[:].indirect(al[:]), fq, A.add), ["fp%d" % b, "fq%d" % b], ["kb%d" % b])
+            if b < 3:
+                op("s", lambda: S.activation(T.zt[:, b:4 * C:4], kb.indirect(al[:]), ACT.Copy, scale=0.5), ["kb%d" % b], ["zt%d" % b])
+        op("s", lambda: S.activation(T.zt[:, 4 * H + 3:4 * C:4], kb.indirect(al[:, 14:28]), ACT.Copy, scale=0.5), ["kb3"], ["zt4"])
+        op("v", lambda: V.tensor_scalar(T.zt[:, 3:4 * H:4], kb.indirect(al[:, 0:14]), 0.5, None, A.mult), ["kb3"], ["zt3"])
+        quantize(T.zq[:], T.zs[:], T.zt[:], ["zt%d" % b for b in range(5)], ["zq"])
+        mm(1, blk("wq", 0), blk("wp", 0), T.zq[:, 0:H], T.zs[:, 0:H], ["wq", "wp", "zq"], H)
+        mm(5, blk("wq", 0), blk("wp", 0), T.zq[:, H:C], T.zs[:, H:C], ["wq", "wp", "zq"], H)
+        for b in range(1, 4):
+            mm(1 + b, blk("wq", b), blk("wp", b), T.zq[:], T.zs[:], ["wq", "wp", "zq"])
+        op("s", lambda: S.activation(T.rr0[:, H:C], ps(5, H), ACT.Copy, scale=0.03125), ["ps5"], ["rr0.b"])
+        for b in range(1, 4):
+            op("s", lambda: S.activation(T["rr%d" % b][:], ps(1 + b), ACT.Copy, scale=0.03125), ["ps%d" % (1 + b)], ["rr%d" % b])
+        if not last:
+            turned_back("bl%d" % nxt, "rw2", [0, 1])
+            make_list("ll%d" % nxt, "bl%d" % nxt, 0)
+            make_list("lr%d" % nxt, "bl%d" % nxt, 1)
+        else:
+            e = tt(slot("f0"), pn, nv, A.is_equal)
+            h = ts(slot("f1"), nv, -1.0, A.mult, 224.0, A.add)
+            e = tt(slot("f2"), e, h, A.mult)
+            tt(sub("bl1", 2), pn, e, A.add)
+            turn(T.rp2[:], ["rp2"], T.bl1[:, 0:C], ["bl1.0", "bl1.1", "bl1.2", "bl1.i"])
+            op("s", lambda: S.activation(T.trf[:], T.rp2[:], ACT.Identity, bias=T.c224[:, 0:1]), ["rp2", "c224"], ["trf"])
+            for i in range(3):
+                lane = (i + 2) % 3
+                dma("y", "st_tr", T.tr[:, C * i:C * i + C], T.trf[lane:128:16, :], ["trf"], ["tr%d" % i])
+        op("v", lambda: V.tensor_scalar(T.rr0[:, 0:H], ps(1, H), 0.03125, None, A.mult), ["ps1"], ["rr0.a"])
+        for b in range(4):
+            rks = ["rr0.a", "rr0.b"] if b == 0 else ["rr%d" % b]
+            op("v", lambda: V.tensor_tensor(T.xn[:, b:4 * C:4], T["rr%d" % b][:].indirect(la2), T["fo%d" % b][:], A.add),
+               rks + ["fo%d" % b, lak2], ["xn%d" % b])
+        quantize(T["q%d" % (k + 1)][:], T["qs%d" % (k + 1)][:], T.xn[:], ["xn%d" % b for b in range(4)], ["q%d" % (k + 1)])
+        if not last:
+            pv, sv, lv, rv = pn, sn, lnew, rnew
+            ts(m3(1), lv, -256.0, A.add)
+            ts(m3(2), rv, -256.0, A.add)
+
+    mm(5, T.vq[:], T.vs[:], T.q3[:, 0:H], T.qs3[:, 0:H], ["vq", "q3"], H)
+    mm(6, T.vq[:], T.vs[:], T.q3[:, H:C], T.qs3[:, H:C], ["vq", "q3"], H)
+    dma("y", "st_oc", T.oc[:, 0:4 * C], T.q3[:, 0:C].bitcast(dt.uint8), ["q3"], ["oc"])
+    for i in range(4):
+        dma("y", "st_osc", T.osc[4 * i:4 * i + 4, :], T.qs3[32 * i:32 * i + 4, 0:C], ["q3"], ["osc%d" % i])
+    op("v", lambda: V.tensor_copy(T.yt[:, 0:H], ps(5, H)), ["ps5"], ["yt.a"])
+    op("s", lambda: S.activation(T.yt[:, H:C], ps(6, H), ACT.Copy), ["ps6"], ["yt.b"])
+    dma("s", "st_y", T.y[:], T.yt[:], ["yt.a", "yt.b"], ["yo"])
+    for sem in sorted(count):
+        wait("g", sem, count[sem])

@@ -26,16 +26,17 @@ _sbuf("zs qs0 qs1 qs2 qs3 as0 as1 as2", C, PLANE)
 _sbuf("pidx", 2, I32)
 _sbuf("ti", 16, I32)
 _sbuf("c224", 8, F32)
-_sbuf("offm0 offm1", 2, U16)
+_sbuf("offm", 4, U16)
 _sbuf("upi lfi rti", 28, I32)
 _sbuf("al0 al1 al2", 28, U16)
-_sbuf("lup la0 la1 la2 la3 ll0 ll1 lr0 lr1", 32, U16)
+_sbuf("lup la0 la1 la2 la3", 32, U16)
+_sbuf("lb0 lb1", 64, U16)
 _sbuf("iot prow rrow ra qrow rrep", 464, BF)
 _sbuf("srow urow", 456, F32)
 _sbuf("nT lrow raa pT lT rT raT raaT pp ppT qa qaa qaaa ql qr qaT qaaT qaaaT qlT qrT repl repr_ replT reprT rp2", C, BF)
 _sbuf("sa sl sr sT saT slT srT ulT urT trf yt rr0 rr1 rr2 rr3", C, F32)
 _sbuf("wu", C, F32)
-_sbuf("wc_ wr wp2", C, BF)
+_sbuf("wc_ wr zr", C, BF)
 _sbuf("ba0 ba1 bl0 bl1", C + 480, BF)
 _sbuf("rw rw2", 512, BF)
 _sbuf("m3 v3", 84, F32)
@@ -43,7 +44,7 @@ _sbuf("cb", 28 * 80, F32)
 _sbuf("fo0 fo1 fo2 fo3 fp0 fp1 fp2 fp3", C, BF)
 _sbuf("fq kb", 4 * C, BF)
 
-SEMAPHORES = (["cv", "cs", "ct", "cg", "sent"] + ["ld_" + k for k in "x u v up lf rt wc ws".split()]
+SEMAPHORES = (["cv", "cs", "ct", "cg", "sent"] + ["ld_" + k for k in "x u v up lf rt wc ws z".split()]
               + ["st_" + k for k in "y oc osc tr".split()] + ["cf%d" % k for k in range(4)] + ["arq%d" % k for k in range(3)] + ["arl%d" % k for k in range(3)])
 
 
@@ -183,10 +184,13 @@ def rank_program(g, core, T, topo):
 
     op("g", lambda: g.iota(T.pidx[:], [[0, 2]], 0, 1), [], ["pidx"])
     memset(T.ones[:], 1.0, ["ones"])
-    op("g", lambda: g.affine_select(T.et0[:], T.ones[:], [[-1, 512]], A.is_equal, 0.0, 0, 4), ["ones"], ["et0"])
     op("g", lambda: g.iota(T.iot[:], [[1, 464]], -224, 0, allow_small_or_imprecise_dtypes=True), [], ["iot"])
+    op("g", lambda: g.affine_select(T.et0[:], T.ones[:], [[-1, 512]], A.is_equal, 0.0, 0, 4), ["ones"], ["et0"])
     for b in range(1, 4):
         memset(T["et%d" % b][:, 0:b], 0.0, ["et%d.0" % b])
+    op("s", lambda: S.activation(T.wu[:], T.iot[:, 0:C], ACT.Copy, scale=0.0), ["iot"], ["wu.0", "wu.1", "wu.i"])
+    op("s", lambda: S.activation(T.zr[:], T.iot[:, 0:C], ACT.Copy, scale=0.0), ["iot"], ["zr"])
+    for b in range(1, 4):
         op("s", lambda: S.activation(T["et%d" % b][:, b:512], T.et0[:, 0:512 - b], ACT.Copy), ["et0"], ["et%d" % b])
     memset(T.ba0[:, 0:C], 0.0, ["ba0.0", "ba0.i"])
     memset(T.rw[:, 0:32], 0.0, ["rw.p0"])
@@ -196,7 +200,8 @@ def rank_program(g, core, T, topo):
     memset(T.srow[:, C:456], -BIGV, ["srow.n"])
     memset(T.urow[:, C:456], BIGV, ["urow.n"])
     memset(T.qrow[:, C:464], 600.0, ["qrow.n"])
-    memset(T.c224[:], 224.0, ["c224"])
+    memset(T.c224[:, 0:4], 224.0, ["c224"])
+    memset(T.c224[:, 4:8], -256.0, ["cm256"])
 
     def tiv(i):
         return T.ti[:, i:i + 1], "ti%d" % i
@@ -209,11 +214,6 @@ def rank_program(g, core, T, topo):
     ts(tiv(5), tiv(1), 480, A.mult)
     ts(tiv(6), tiv(2), 464, A.mult)
     ts(tiv(7), tiv(3), -928, A.mult)
-    tt(tiv(8), tiv(4), tiv(5), A.add)
-    tt(tiv(9), tiv(6), tiv(7), A.add)
-    tt(tiv(10), tiv(8), tiv(9), A.add)
-    for h in range(2):
-        ts((T.offm0[:, h:h + 1], "offm0"), tiv(10), 256 * h, A.add, 927, A.min)
 
     def turned_back(big, rw, lanes, between=None):
         turn(T[rw][:, 32:480], [rw], T[big][:, 0:C], ["%s.%s" % (big, k) for k in lanes] + [big + ".i"])
@@ -221,34 +221,50 @@ def rank_program(g, core, T, topo):
             between()
         turn(T[big][:, C:928], [big + ".s"], T[rw][:, 16:496], [rw, rw + ".p0", rw + ".p1"])
 
-    def make_list(out, big, lane):
-        op("v", lambda: V.tensor_scalar(T[out][:], T[big][:, 0:928].indirect(T["offm%d" % lane][:]), 224.0, None, A.add),
-           ["%s.%d" % (big, lane), big + ".i", big + ".s", "offm%d" % lane], [out])
+    def make_list(out, big, lanes):
+        op("v", lambda: V.tensor_scalar(T[out][:], T[big][:, 0:928].indirect(T.offm[:, 0:2 * len(lanes)]), 224.0, None, A.add),
+           ["%s.%d" % (big, i) for i in lanes] + [big + ".i", big + ".s"] + ["offm%d" % i for i in lanes], [out])
 
-    nv = plane("nT", 0)
-    turned("nT", "iot")
     op("v", lambda: V.tensor_copy(T.lup[:, 0:28], T.upi[:]), ["upi"], ["lup"])
+    op("v", lambda: V.tensor_copy(T.lb0[:, 32:60], T.rti[:]), ["rti"], ["lb0.r"])
+    op("v", lambda: V.tensor_copy(T.lb0[:, 0:28], T.lfi[:]), ["lfi"], ["lb0.l"])
     lup = T.lup[:, 0:28]
     gather("v", (T.prow[:, 0:C], "prow"), T.iot[:], ["iot"], lup, "lup")
-    op("v", lambda: V.tensor_copy(T.lr0[:, 0:28], T.rti[:]), ["rti"], ["lr0"])
-    op("v", lambda: V.tensor_copy(T.ll0[:, 0:28], T.lfi[:]), ["lfi"], ["ll0"])
-    gather("s", (T.rrow[:, 0:C], "rrow"), T.iot[:], ["iot"], T.lr0[:, 0:28], "lr0")
-    gather("s", row("lrow"), T.iot[:], ["iot"], T.ll0[:, 0:28], "ll0")
+    gather("s", (T.rrow[:, 0:C], "rrow"), T.iot[:], ["iot"], T.lb0[:, 32:60], "lb0.r")
+    gather("s", row("lrow"), T.iot[:], ["iot"], T.lb0[:, 0:28], "lb0.l")
     gather("s", (T.ra[:, 0:C], "ra"), T.rrow[:], ["rrow", "rrow.n"], lup, "lup")
-    gather("s", row("raa"), T.ra[:], ["ra", "ra.n"], lup, "lup")
-    gather("s", row("pp"), T.prow[:], ["prow", "prow.n"], lup, "lup")
+    tt(tiv(8), tiv(4), tiv(5), A.add)
+    tt(tiv(9), tiv(6), tiv(7), A.add)
     turned("pT", "prow")
+    tt(tiv(10), tiv(8), tiv(9), A.add)
+    nv = plane("nT", 0)
+    turned("nT", "iot")
     pT = plane("pT", 0)
     e = ts(slot("i0"), pT, 224.0, A.is_equal)
     f_ = tt(slot("i1"), nv, pT, A.subtract)
+    ts((T.offm[:, 0:1], "offm0"), tiv(10), 0, A.add, 927, A.min)
     f_ = tt(slot("i2"), e, f_, A.mult)
+    ts((T.offm[:, 1:2], "offm0"), tiv(10), 256, A.add, 927, A.min)
     tt(sub("ba0", 0), pT, f_, A.add)
-    for b in range(4):
+
+    def quantize_constants(b):
         quantize(blk("eq", b), blk("es", b), T["et%d" % b][:], ["et%d" % b] + (["et%d.0" % b] if b else []), ["eq%d" % b])
-        if b == 0:
-            turned_back("ba0", "rw", [0])
-        if b == 1:
-            make_list("la0", "ba0", 0)
+    ts((T.offm[:, 2:3], "offm1"), tiv(10), 1, A.add, 927, A.min)
+    turned_back("ba0", "rw", [0], lambda: ts((T.offm[:, 3:4], "offm1"), tiv(10), 257, A.add, 927, A.min))
+    quantize_constants(0)
+    make_list("la0", "ba0", [0])
+    for b in range(1, 4):
+        quantize_constants(b)
+    quantize(T.uq[:], T.us[:], T.ut[:], ["ut"], ["uq"])
+    zeros = {"wc_": ["wc_.0", "wc_.i"], "ba1": ["ba1.0", "ba1.i"], "wr": ["wr.0", "wr.i"],
+             "bl1": ["bl1.0", "bl1.1", "bl1.2", "bl1.i"], "bl0": ["bl0.0", "bl0.1", "bl0.2", "bl0.i"]}
+    for k in zeros:
+        dma("y", "ld_z", T[k][:, 0:C], T.zr[:], ["zr"], [])
+    for k in zeros:
+        for key in zeros[k]:
+            writer[key] = ("ld_z", count["ld_z"], "y")
+    facts[("ld_z", count["ld_z"])] = {}
+    quantize(T.q0[:], T.qs0[:], T.xt[:], ["xt"], ["q0"])
     turned("rT", "rrow")
     turned("lT", "lrow")
     lv, rv = plane("lT", 0), plane("rT", 0)
@@ -261,39 +277,30 @@ def rank_program(g, core, T, topo):
     ts(m3(0), nv, -256.0, A.add)
     ts(m3(1), lv, -256.0, A.add)
     ts(m3(2), rv, -256.0, A.add)
-    memset(T.wu[:], 0.0, ["wu.0", "wu.1", "wu.i"])
-    memset(T.wc_[:], 0.0, ["wc_.0", "wc_.i"])
-    quantize(T.q0[:], T.qs0[:], T.xt[:], ["xt"], ["q0"])
-    quantize(T.uq[:], T.us[:], T.ut[:], ["ut"], ["uq"])
-    for h in range(2):
-        ts((T.offm1[:, h:h + 1], "offm1"), tiv(10), 256 * h + 1, A.add, 927, A.min)
-    memset(T.ba1[:, 0:C], 0.0, ["ba1.0", "ba1.i"])
 
     def late_constants():
         memset(T.rrep[:, C:464], 224.0, ["rrep.n"])
-        memset(T.wr[:], 0.0, ["wr.0", "wr.i"])
-
-    def later_constants():
-        memset(T.wp2[:], 0.0, ["wp2.1", "wp2.2", "wp2.i"])
         memset(T.rw2[:, 0:32], 0.0, ["rw2.p0"])
         memset(T.rw2[:, 480:512], 0.0, ["rw2.p1"])
-        memset(T.bl0[:, 0:C], 0.0, ["bl0.0", "bl0.1", "bl0.i"])
-        memset(T.bl1[:, 0:C], 0.0, ["bl1.0", "bl1.1", "bl1.2", "bl1.i"])
 
     def derive(k, pv, sv, lv, rv):
         def add(f, *a):
             todo.append(lambda: f(*a))
-        ppv, spv = plane("ppT", 1), plane("ppT", 2)
+        spv = slot("sp")
         if k == 0:
-            ppv, spv = plane("ppT", 0), slot("sp0")
+            ppv = plane("ppT", 0)
             for n in ("raT raaT ppT").split():
                 add(turned, n, n[:-1])
             add(tt, sv, plane("raT", 0), nv, A.is_equal)
             add(tt, spv, plane("raaT", 0), pv, A.is_equal)
             add(ts, slot("d0"), ppv, 224.0, A.is_equal)
         else:
+            ppv = plane("ppT", 2)
             add(turned, "ppT", "pp")
+            add(tt, sv, plane("ppT", 0), nv, A.not_equal)
             add(tt, slot("d0"), ppv, pv, A.is_equal)
+            add(turned, "raaT", "raa")
+            add(tt, spv, plane("raaT", 0), pv, A.not_equal)
         add(tt, slot("d1"), nv, ppv, A.subtract)
         add(tt, slot("d2"), sv, spv, A.is_equal)
         add(tt, slot("d3"), lv, rv, A.subtract)
@@ -305,18 +312,16 @@ def rank_program(g, core, T, topo):
         add(tt, slot("d8"), rv, slot("d6"), A.add)
         add(tt, slot("dz"), slot("d7"), pv, A.subtract)
         add(tt, slot("cn"), slot("d8"), nv, A.subtract)
-        add(tt, slot("sd"), spv, sv, A.subtract)
-        add(ts, slot("s2"), sv, -2.0, A.mult, 1.0, A.add)
 
-    pv, sv = sub("ba0", 0), slot("side0")
+    pv, sv = sub("ba0", 0), slot("side")
     for k in range(3):
         par, nxt = k % 2, 1 - k % 2
         last = k == 2
         q, qs, qk = T["q%d" % k], T["qs%d" % k], "q%d" % k
         dst = T.cores[(rank + STEP[k]) % N]
         la, lak = T["la%d" % k][:, 0:28], "la%d" % k
-        ll, llk = T["ll%d" % par][:, 0:28], "ll%d" % par
-        lr, lrk = T["lr%d" % par][:, 0:28], "lr%d" % par
+        ll, llk = T["lb%d" % par][:, 0:28], ["lb%d" % par, "lb0.l"][k == 0]
+        lr, lrk = T["lb%d" % par][:, 32:60], ["lb%d" % par, "lb0.r"][k == 0]
         lak2 = "la%d" % (k + 1)
         la2 = T[lak2][:, 0:28]
         send(dst, "arq%d" % k, T["aq%d" % k][:, 0:C].bitcast(dt.uint8), q[:, 0:C].bitcast(dt.uint8), [qk])
@@ -325,17 +330,26 @@ def rank_program(g, core, T, topo):
         mm(7, T.uq[:], T.us[:], q[:, H:C], qs[:, H:C], ["uq", qk], H)
         for b in range(4):
             mm(1 + b, blk("eq", b), blk("es", b), q[:], qs[:], ["eq%d" % b, qk])
+        if k:
+            derive(k, pv, sv, lv, rv)
+            fill(3)
         op("v", lambda: V.tensor_copy(T.srow[:, 0:H], ps(0, H)), ["ps0"], ["srow.a"])
         op("s", lambda: S.activation(T.srow[:, H:C], ps(7, H), ACT.Copy), ["ps7"], ["srow.b"])
         sk = ["srow.a", "srow.b", "srow.n"]
         gather("s", row("sl"), T.srow[:, 0:456], sk, ll, llk)
         gather("s", row("sr"), T.srow[:, 0:456], sk, lr, lrk)
         if k:
-            turn(T.rp2[:], ["rp2"], T.wp2[:], ["wp2.1", "wp2.2", "wp2.i"])
-            gather("s", row("pp"), T.rp2[:], ["rp2"], la, lak)
-        for b in range(4):
+            for i, w in ((1, lv), (2, rv)):
+                op("s", lambda: S.activation(m3(i)[0], w[0], ACT.Identity, bias=T.c224[:, 4:5]), [w[1], "cm256"], [m3(i)[1]])
+        else:
+            gather("s", row("raa"), T.ra[:], ["ra", "ra.n"], lup, "lup")
+            gather("s", row("pp"), T.prow[:], ["prow", "prow.n"], lup, "lup")
+        for b in range(3):
             op("s", lambda: S.activation(T["fo%d" % b][:], ps(1 + b), ACT.Copy), ["ps%d" % (1 + b)], ["fo%d" % b])
-        derive(k, pv, sv, lv, rv)
+        if k:
+            fill(2)
+        else:
+            derive(k, pv, sv, lv, rv)
         gather("v", row("sa"), T.srow[:, 0:456], sk, la, lak)
         turn(T.sT[:], ["sT"], T.srow[:, 0:C], sk)
         turned("saT", "sa")
@@ -404,30 +418,31 @@ def rank_program(g, core, T, topo):
         yq = tt(slot("yq"), Qa, pv, A.subtract)
         yl = tt(slot("yl"), xl, eL, A.mult)
         turned("qaaT", "qaa")
-        xr = tt(slot("xra"), xr, eA, A.mult)
-        YL = tt(slot("YL"), yl, eA, A.mult)
+        t = tt(slot("r0"), Qa, nv, A.subtract)
         eB = tt(slot("eB"), Qaa, Qa, A.is_equal)
         rot = tt(slot("rot"), rn, eB, A.mult)
         xb = tt(slot("xb"), xp, eB, A.mult)
         turned("qrT", "qr")
         rd = tt(slot("rd"), rot, slot("dz"), A.mult)
-        xbd = tt(slot("xbd"), xb, slot("dz"), A.mult)
         eR = tt(slot("eR"), Qr, Qa, A.is_equal)
+        xbd = tt(slot("xbd"), xb, slot("dz"), A.mult)
+        yr = tt(slot("yr"), xr, eR, A.mult)
         rd = tt(slot("rd2"), rd, pv, A.add)
-        YR = tt(slot("YR"), xr, eR, A.mult)
-        Y = tt(slot("Y"), YL, YR, A.add)
-        yd = tt(slot("yd"), Y, yq, A.mult)
-        base = tt(slot("base"), rd, yd, A.add)
-        turned("qaaaT", "qaaa")
-        eC = tt(slot("eC"), Qaaa, Qa, A.is_equal)
-        t = tt(slot("r0"), Qa, nv, A.subtract)
-        cd = tt(slot("cd"), xbd, eC, A.mult)
+        yy = tt(slot("yy"), yl, yr, A.add)
         fr = tt(slot("r1"), rot, slot("cn"), A.mult)
-        pn = tt(sub("ba%d" % nxt, 0), base, cd, A.add)
+        Y = tt(slot("Y"), yy, eA, A.mult)
+        rs1 = tt(slot("rs1"), rot, sv, A.mult)
+        yd = tt(slot("yd"), Y, yq, A.mult)
+        turned("qaaaT", "qaaa")
+        base = tt(slot("base"), rd, yd, A.add)
+        eC = tt(slot("eC"), Qaaa, Qa, A.is_equal)
         t = tt(slot("r2"), Y, t, A.mult)
-        turned_back("ba%d" % nxt, "rw", [0], lambda: tt(slot("r3"), fr, nv, A.add))
-        tt(sub("wr", 0), slot("r3"), t, A.add)
-        make_list(lak2, "ba%d" % nxt, 0)
+        cd = tt(slot("cd"), xbd, eC, A.mult)
+        fr = tt(slot("r3"), fr, nv, A.add)
+        pn = tt(sub("ba%d" % nxt, 0), base, cd, A.add)
+        rs0 = tt(slot("rs0"), rot, rs1, A.subtract)
+        turned_back("ba%d" % nxt, "rw", [0], lambda: tt(sub("wr", 0), fr, t, A.add))
+        make_list(lak2, "ba%d" % nxt, [0])
         send(dst, "arl%d" % k, T["al%d" % k][:], la2, [lak2])
         wait("t", "arq%d" % k, 2 * len(topo.engines(core, dst)))
         fbank = [5, 6, 7, 0]
@@ -436,28 +451,13 @@ def rank_program(g, core, T, topo):
         for b in range(4):
             op("s", lambda: S.activation(T["fp%d" % b][:], ps(fbank[b]), ACT.Copy), ["ps%d" % fbank[b]], ["fp%d" % b])
             dma("y", "cf%d" % b, T.fq[:, C * b:C * b + C], T["fp%d" % b][:], ["fp%d" % b], ["fq%d" % b])
-        isc = tt(slot("isc"), xb, eC, A.mult)
-        rs1 = tt(slot("rs1"), rot, sv, A.mult)
         turn(T.rrep[:, 0:C], ["rrep"], T.wr[:], ["wr.0", "wr.i"])
         rk = ["rrep", "rrep.n"]
         gather("s", row("repl"), T.rrep[:], rk, ll, llk)
-        gather("s", row("repr_"), T.rrep[:], rk, lr, lrk)
-        rs0 = tt(slot("rs0"), rot, rs1, A.subtract)
+        gather("v", row("repr_"), T.rrep[:], rk, lr, lrk)
         if not last:
-            t1 = tt(slot("s3"), rot, slot("sd"), A.mult)
-            t2 = tt(slot("s4"), isc, slot("s2"), A.mult)
-            t3 = tt(slot("s5"), Y, sv, A.mult)
-            t1 = tt(slot("s6"), sv, t1, A.add)
-            t3 = tt(slot("s7"), YL, t3, A.subtract)
-            t1 = tt(slot("s8"), t1, t2, A.add)
-            sn = tt(slot("side%d" % nxt), t1, t3, A.add)
-        else:
-            quantize(T.vq[:], T.vs[:], T.vt[:], ["vt"], ["vq"])
-        if k == 0:
-            later_constants()
-        if not last:
-            ts(sub("wp2", 1), pn, 0.0, A.add)
-            ts(sub("wp2", 2), sn, 0.0, A.add)
+            bl2 = sub("bl%d" % nxt, 2)
+            op("s", lambda: S.activation(bl2[0], pn[0], ACT.Copy), [pn[1]], [bl2[1]])
         turned("replT", "repl")
         turned("reprT", "repr_")
         Rl, Rr = plane("replT", 0), plane("reprT", 0)
@@ -468,6 +468,8 @@ def rank_program(g, core, T, topo):
         t2 = tt(slot("l3"), rs0, t2, A.mult)
         tt(lnew, Rl, t1, A.add)
         tt(rnew, Rr, t2, A.add)
+        if last:
+            quantize(T.vq[:], T.vs[:], T.vt[:], ["vt"], ["vq"])
         wait("v", "arl%d" % k, len(topo.engines(core, dst)))
         wait("s", "arl%d" % k, len(topo.engines(core, dst)))
         al = T["al%d" % k]
@@ -481,15 +483,19 @@ def rank_program(g, core, T, topo):
         quantize(T.zq[:], T.zs[:], T.zt[:], ["zt%d" % b for b in range(5)], ["zq"])
         mm(1, blk("wq", 0), blk("wp", 0), T.zq[:, 0:H], T.zs[:, 0:H], ["wq", "wp", "zq"], H)
         mm(5, blk("wq", 0), blk("wp", 0), T.zq[:, H:C], T.zs[:, H:C], ["wq", "wp", "zq"], H)
+        wbank = [1, 2, 3, 6]
         for b in range(1, 4):
-            mm(1 + b, blk("wq", b), blk("wp", b), T.zq[:], T.zs[:], ["wq", "wp", "zq"])
+            mm(wbank[b], blk("wq", b), blk("wp", b), T.zq[:], T.zs[:], ["wq", "wp", "zq"])
+        op("s", lambda: S.activation(T.rr0[:, 0:H], ps(1, H), ACT.Copy, scale=0.03125), ["ps1"], ["rr0.a"])
         op("s", lambda: S.activation(T.rr0[:, H:C], ps(5, H), ACT.Copy, scale=0.03125), ["ps5"], ["rr0.b"])
         for b in range(1, 4):
-            op("s", lambda: S.activation(T["rr%d" % b][:], ps(1 + b), ACT.Copy, scale=0.03125), ["ps%d" % (1 + b)], ["rr%d" % b])
+            op("s", lambda: S.activation(T["rr%d" % b][:], ps(wbank[b]), ACT.Copy, scale=0.03125), ["ps%d" % wbank[b]], ["rr%d" % b])
+        gather("s", row("sa"), T.rr3[:], ["rr3"], la2, lak2)
         if not last:
-            turned_back("bl%d" % nxt, "rw2", [0, 1])
-            make_list("ll%d" % nxt, "bl%d" % nxt, 0)
-            make_list("lr%d" % nxt, "bl%d" % nxt, 1)
+            turned_back("bl%d" % nxt, "rw2", [0, 1, 2])
+            make_list("lb%d" % nxt, "bl%d" % nxt, [0, 1])
+            gather("s", row("pp"), T.rw2[:, 32:480], ["rw2"], la2, lak2)
+            gather("s", row("raa"), T.pp[:], ["pp"], la2, lak2)
         else:
             e = tt(slot("f0"), pn, nv, A.is_equal)
             h = ts(slot("f1"), nv, -1.0, A.mult, 224.0, A.add)
@@ -500,16 +506,14 @@ def rank_program(g, core, T, topo):
             for i in range(3):
                 lane = (i + 2) % 3
                 dma("y", "st_tr", T.tr[:, C * i:C * i + C], T.trf[lane:128:16, :], ["trf"], ["tr%d" % i])
-        op("v", lambda: V.tensor_scalar(T.rr0[:, 0:H], ps(1, H), 0.03125, None, A.mult), ["ps1"], ["rr0.a"])
-        for b in range(4):
+        for b in range(3):
             rks = ["rr0.a", "rr0.b"] if b == 0 else ["rr%d" % b]
             op("v", lambda: V.tensor_tensor(T.xn[:, b:4 * C:4], T["rr%d" % b][:].indirect(la2), T["fo%d" % b][:], A.add),
                rks + ["fo%d" % b, lak2], ["xn%d" % b])
+        tt((T.xn[:, 3:4 * C:4], "xn3"), row("sa"), (ps(4), "ps4"), A.add)
         quantize(T["q%d" % (k + 1)][:], T["qs%d" % (k + 1)][:], T.xn[:], ["xn%d" % b for b in range(4)], ["q%d" % (k + 1)])
         if not last:
-            pv, sv, lv, rv = pn, sn, lnew, rnew
-            ts(m3(1), lv, -256.0, A.add)
-            ts(m3(2), rv, -256.0, A.add)
+            pv, lv, rv = pn, lnew, rnew
 
     mm(5, T.vq[:], T.vs[:], T.q3[:, 0:H], T.qs3[:, 0:H], ["vq", "q3"], H)
     mm(6, T.vq[:], T.vs[:], T.q3[:, H:C], T.qs3[:, H:C], ["vq", "q3"], H)

from concourse.mybir import dt, AluOpType, ActivationFunctionType

N = 4
C = 448
H = 224
STEP = [1, 2, 3]
BIGV = 3.0e29

F32, BF, U16, I32, CODE, PLANE = "float32", "bfloat16", "uint16", "int32", "float8_e4m3fn_x4", "uint8"
SCRATCH = {"ps": ("psum", [128, 4096], F32)}


def _sbuf(names, n, dtype):
    for k in names.split():
        SCRATCH[k] = ("sbuf", [128, n], dtype)


_sbuf("xt xn zt", 4 * C, BF)
_sbuf("ut vt ones et0 et1 et2 et3", 512, BF)
_sbuf("uq vq", 128, CODE)
_sbuf("us vs", 128, PLANE)
_sbuf("wq eq", 512, CODE)
_sbuf("wp es", 512, PLANE)
_sbuf("zq q0 q1 q2 q3 aq0 aq1 aq2", C, CODE)
_sbuf("zs qs0 qs1 qs2 qs3 as0 as1 as2", C, PLANE)
_sbuf("pidx", 2, I32)
_sbuf("ti", 16, I32)
_sbuf("c224", 8, F32)
_sbuf("offm", 4, U16)
_sbuf("upi lfi rti", 28, I32)
_sbuf("al0 al1 al2", 28, U16)
_sbuf("lup la0 la1 la2 la3", 32, U16)
_sbuf("lb0 lb1", 64, U16)
_sbuf("iot prow rrow ra qrow rrep", 464, BF)
_sbuf("srow urow", 456, F32)
_sbuf("nT lrow raa pT lT rT raT raaT pp ppT qa qaa qaaa ql qr qaT qaaT qaaaT qlT qrT repl repr_ replT reprT rp2", C, BF)
_sbuf("sa sl sr sT saT slT srT ulT urT trf yt rr0 rr1 rr2 rr3", C, F32)
_sbuf("wu", C, F32)
_sbuf("wc_ wr zr", C, BF)
_sbuf("ba0 ba1 bl0 bl1", C + 480, BF)
_sbuf("rw rw2", 512, BF)
_sbuf("m3 v3", 84, F32)
_sbuf("cb", 28 * 80, F32)
_sbuf("fo0 fo1 fo2 fo3 fp0 fp1 fp2 fp3", C, BF)
_sbuf("fq kb", 4 * C, BF)

SEMAPHORES = (["cv", "cs", "ct", "cg", "sent"] + ["ld_" + k for k in "x u v up lf rt wc ws z".split()]
              + ["st_" + k for k in "y oc osc tr".split()] + ["cf%d" % k for k in range(4)] + ["arq%d" % k for k in range(3)] + ["arl%d" % k for k in range(3)])


def rank_program(g, core, T, topo):
    rank = T.rank_of(core)
    if rank is None:
        return
    A = AluOpType
    ACT = ActivationFunctionType
    V, S = g.vector, g.scalar
    queue = {"v": V, "s": S, "t": g.tensor, "g": g, "y": g.sync}

    count = {}
    seen = {k: {} for k in queue}
    facts = {}
    writer, readers = {}, {}

    def wait(q, sem, val):
        s = seen[q]
        if s.get(sem, 0) >= val:
            return
        queue[q].wait_ge(T.sem[sem], val)
        s[sem] = val
        for k, n in facts.get((sem, val), {}).items():
            if s.get(k, 0) < n:
                s[k] = n

    def prepare(q, reads, writes):
        need = {}
        for k in reads + writes:
            if k in writer:
                w, n, wq = writer[k]
                need[w] = max(need.get(w, 0), n)
        for k in writes:
            for w, n, rq in readers.get(k, []):
                if rq != q or w[0] != "c":
                    need[w] = max(need.get(w, 0), n)
        own = "c" + q
        for w in sorted(need, key=lambda w: (w == own, w)):
            wait(q, w, need[w])

    def note(q, sem, val, reads, writes):
        facts[(sem, val)] = dict(seen[q])
        for k in writes:
            writer[k] = (sem, val, q)
            readers[k] = []
        for k in reads:
            readers.setdefault(k, []).append((sem, val, q))

    def op(q, fn, reads, writes):
        prepare(q, reads, writes)
        sem = "c" + q
        count[sem] = count.get(sem, 0) + 1
        fn().then_inc(T.sem[sem], 1)
        note(q, sem, count[sem], reads, writes)

    def dma(q, sem, out, in_, reads, writes):
        prepare(q, reads, writes)
        count[sem] = count.get(sem, 0) + 16
        queue[q].dma_start(out, in_).then_inc(T.sem[sem], 16)
        note(q, sem, count[sem], reads, writes)

    def send(dst, rsem, out, in_, reads):
        prepare("g", reads, [])
        rid, pid, se = topo.addr(dst)
        g.remote_dma(out, in_, T.sem[rsem], T.sem["sent"], pid, rid, topo.mask(core, dst))
        count["sent"] = count.get("sent", 0) + len(topo.engines(core, dst))

    def ps(b, n=C):
        return T.ps[:, 512 * b:512 * b + n]

    slots = {}

    def slot(name):
        i = slots.setdefault(name, len(slots))
        return T.cb[:, 28 * i:28 * i + 28], "cb." + name

    def plane(buf, lane):
        return T[buf][:, lane:C:16], buf

    def sub(buf, lane):
        return T[buf][:, lane:C:16], "%s.%d" % (buf, lane)

    def tt(out, a, b, o):
        op("v", lambda: V.tensor_tensor(out[0], a[0], b[0], o), [a[1], b[1]], [out[1]])
        return out

    def ts(out, a, s1, o1, s2=None, o2=None):
        if o2 is None:
            op("v", lambda: V.tensor_scalar(out[0], a[0], s1, None, o1), [a[1]], [out[1]])
        else:
            op("v", lambda: V.tensor_scalar(out[0], a[0], s1, s2, o1, o2), [a[1]], [out[1]])
        return out

    def turn(out, ok, in_, ik):
        op("v", lambda: V.transpose(out, in_), ik, ok)

    def turned(out, in_):
        turn(T[out][:], [out], T[in_][:, 0:C], [in_])

    def gather(q, out, win, wk, off, fk):
        if q == "s":
            op("s", lambda: S.activation(out[0], win.indirect(off), ACT.Copy), wk + [fk], [out[1]])
        else:
            op("v", lambda: V.tensor_copy(out[0], win.indirect(off)), wk + [fk], [out[1]])

    def row(buf):
        return T[buf][:], buf

    def memset(ap, val, keys):
        op("v", lambda: V.memset(ap, val), [], keys)

    def mm(bank, l, ls, r, rs, keys, n=C):
        op("t", lambda: g.tensor.matmul_mx(ps(bank, n), l, ls, r, rs, True, True), keys, ["ps%d" % bank])

    def quantize(out, os, in_, reads, writes):
        op("v", lambda: V.quantize_mx(out, os, in_), reads, writes)

    def blk(buf, b):
        return T[buf][:, 128 * b:128 * b + 128]

    todo = []

    def fill(n=1):
        for _ in range(n):
            if todo:
                todo.pop(0)()

    dma("y", "ld_up", T.upi[:], T.up[:], [], ["upi"])
    dma("s", "ld_rt", T.rti[:], T.rt[:], [], ["rti"])
    dma("s", "ld_lf", T.lfi[:], T.lf[:], [], ["lfi"])
    dma("y", "ld_x", T.xt[:], T.x[:], [], ["xt"])
    dma("y", "ld_u", T.ut[:], T.u[:], [], ["ut"])
    dma("y", "ld_wc", T.wq[:, 0:512].bitcast(dt.uint8), T.wc[:], [], ["wq"])
    dma("y", "ld_ws", T.wp[:, 0:512], T.ws[:], [], ["wp"])
    dma("y", "ld_v", T.vt[:], T.v[:], [], ["vt"])

    op("g", lambda: g.iota(T.pidx[:], [[0, 2]], 0, 1), [], ["pidx"])
    memset(T.ones[:], 1.0, ["ones"])
    op("g", lambda: g.iota(T.iot[:], [[1, 464]], -224, 0, allow_small_or_imprecise_dtypes=True), [], ["iot"])
    op("g", lambda: g.affine_select(T.et0[:], T.ones[:], [[-1, 512]], A.is_equal, 0.0, 0, 4), ["ones"], ["et0"])
    for b in range(1, 4):
        memset(T["et%d" % b][:, 0:b], 0.0, ["et%d.0" % b])
    op("s", lambda: S.activation(T.wu[:], T.iot[:, 0:C], ACT.Copy, scale=0.0), ["iot"], ["wu.0", "wu.1", "wu.i"])
    op("s", lambda: S.activation(T.zr[:], T.iot[:, 0:C], ACT.Copy, scale=0.0), ["iot"], ["zr"])
    for b in range(1, 4):
        op("s", lambda: S.activation(T["et%d" % b][:, b:512], T.et0[:, 0:512 - b], ACT.Copy), ["et0"], ["et%d" % b])
    memset(T.ba0[:, 0:C], 0.0, ["ba0.0", "ba0.i"])
    memset(T.rw[:, 0:32], 0.0, ["rw.p0"])
    memset(T.rw[:, 480:512], 0.0, ["rw.p1"])
    for k in ("prow", "rrow", "ra"):
        memset(T[k][:, C:464], 224.0, [k + ".n"])
    memset(T.srow[:, C:456], -BIGV, ["srow.n"])
    memset(T.urow[:, C:456], BIGV, ["urow.n"])
    memset(T.qrow[:, C:464], 600.0, ["qrow.n"])
    memset(T.c224[:, 0:4], 224.0, ["c224"])
    memset(T.c224[:, 4:8], -256.0, ["cm256"])

    def tiv(i):
        return T.ti[:, i:i + 1], "ti%d" % i
    pd = (T.pidx[:, 0:1], "pidx")
    ts(tiv(0), pd, 1, A.logical_shift_right, 7, A.bitwise_and)
    ts(tiv(1), pd, 1, A.bitwise_and)
    ts(tiv(2), pd, 4, A.logical_shift_right, 1, A.bitwise_and)
    ts(tiv(4), tiv(0), 32, A.mult)
    tt(tiv(3), tiv(1), tiv(2), A.mult)
    ts(tiv(5), tiv(1), 480, A.mult)
    ts(tiv(6), tiv(2), 464, A.mult)
    ts(tiv(7), tiv(3), -928, A.mult)

    def turned_back(big, rw, lanes, between=None):
        turn(T[rw][:, 32:480], [rw], T[big][:, 0:C], ["%s.%s" % (big, k) for k in lanes] + [big + ".i"])
        if between:
            between()
        turn(T[big][:, C:928], [big + ".s"], T[rw][:, 16:496], [rw, rw + ".p0", rw + ".p1"])

    def make_list(out, big, lanes):
        op("v", lambda: V.tensor_scalar(T[out][:], T[big][:, 0:928].indirect(T.offm[:, 0:2 * len(lanes)]), 224.0, None, A.add),
           ["%s.%d" % (big, i) for i in lanes] + [big + ".i", big + ".s"] + ["offm%d" % i for i in lanes], [out])

    op("v", lambda: V.tensor_copy(T.lup[:, 0:28], T.upi[:]), ["upi"], ["lup"])
    op("v", lambda: V.tensor_copy(T.lb0[:, 32:60], T.rti[:]), ["rti"], ["lb0.r"])
    op("v", lambda: V.tensor_copy(T.lb0[:, 0:28], T.lfi[:]), ["lfi"], ["lb0.l"])
    lup = T.lup[:, 0:28]
    gather("v", (T.prow[:, 0:C], "prow"), T.iot[:], ["iot"], lup, "lup")
    gather("s", (T.rrow[:, 0:C], "rrow"), T.iot[:], ["iot"], T.lb0[:, 32:60], "lb0.r")
    gather("s", row("lrow"), T.iot[:], ["iot"], T.lb0[:, 0:28], "lb0.l")
    gather("s", (T.ra[:, 0:C], "ra"), T.rrow[:], ["rrow", "rrow.n"], lup, "lup")
    tt(tiv(8), tiv(4), tiv(5), A.add)
    tt(tiv(9), tiv(6), tiv(7), A.add)
    turned("pT", "prow")
    tt(tiv(10), tiv(8), tiv(9), A.add)
    nv = plane("nT", 0)
    turned("nT", "iot")
    pT = plane("pT", 0)
    e = ts(slot("i0"), pT, 224.0, A.is_equal)
    f_ = tt(slot("i1"), nv, pT, A.subtract)
    ts((T.offm[:, 0:1], "offm0"), tiv(10), 0, A.add, 927, A.min)
    f_ = tt(slot("i2"), e, f_, A.mult)
    ts((T.offm[:, 1:2], "offm0"), tiv(10), 256, A.add, 927, A.min)
    tt(sub("ba0", 0), pT, f_, A.add)

    def quantize_constants(b):
        quantize(blk("eq", b), blk("es", b), T["et%d" % b][:], ["et%d" % b] + (["et%d.0" % b] if b else []), ["eq%d" % b])
    ts((T.offm[:, 2:3], "offm1"), tiv(10), 1, A.add, 927, A.min)
    turned_back("ba0", "rw", [0], lambda: ts((T.offm[:, 3:4], "offm1"), tiv(10), 257, A.add, 927, A.min))
    quantize_constants(0)
    make_list("la0", "ba0", [0])
    for b in range(1, 4):
        quantize_constants(b)
    quantize(T.uq[:], T.us[:], T.ut[:], ["ut"], ["uq"])
    zeros = {"wc_": ["wc_.0", "wc_.i"], "ba1": ["ba1.0", "ba1.i"], "wr": ["wr.0", "wr.i"],
             "bl1": ["bl1.0", "bl1.1", "bl1.2", "bl1.i"], "bl0": ["bl0.0", "bl0.1", "bl0.2", "bl0.i"]}
    for k in zeros:
        dma("y", "ld_z", T[k][:, 0:C], T.zr[:], ["zr"], [])
    for k in zeros:
        for key in zeros[k]:
            writer[key] = ("ld_z", count["ld_z"], "y")
    facts[("ld_z", count["ld_z"])] = {}
    quantize(T.q0[:], T.qs0[:], T.xt[:], ["xt"], ["q0"])
    turned("rT", "rrow")
    turned("lT", "lrow")
    lv, rv = plane("lT", 0), plane("rT", 0)

    def m3(i):
        return T.m3[:, 28 * i:28 * i + 28], "m3.%d" % i

    def v3(i):
        return T.v3[:, 28 * i:28 * i + 28], "v3.%d" % i
    ts(m3(0), nv, -256.0, A.add)
    ts(m3(1), lv, -256.0, A.add)
    ts(m3(2), rv, -256.0, A.add)

    def late_constants():
        memset(T.rrep[:, C:464], 224.0, ["rrep.n"])
        memset(T.rw2[:, 0:32], 0.0, ["rw2.p0"])
        memset(T.rw2[:, 480:512], 0.0, ["rw2.p1"])

    def derive(k, pv, sv, lv, rv):
        def add(f, *a):
            todo.append(lambda: f(*a))
        spv = slot("sp")
        if k == 0:
            ppv = plane("ppT", 0)
            for n in ("raT raaT ppT").split():
                add(turned, n, n[:-1])
            add(tt, sv, plane("raT", 0), nv, A.is_equal)
            add(tt, spv, plane("raaT", 0), pv, A.is_equal)
            add(ts, slot("d0"), ppv, 224.0, A.is_equal)
        else:
            ppv = plane("ppT", 2)
            add(turned, "ppT", "pp")
            add(tt, sv, plane("ppT", 0), nv, A.not_equal)
            add(tt, slot("d0"), ppv, pv, A.is_equal)
            add(turned, "raaT", "raa")
            add(tt, spv, plane("raaT", 0), pv, A.not_equal)
        add(tt, slot("d1"), nv, ppv, A.subtract)
        add(tt, slot("d2"), sv, spv, A.is_equal)
        add(tt, slot("d3"), lv, rv, A.subtract)
        add(tt, slot("d4"), slot("d0"), slot("d1"), A.mult)
        add(ts, slot("d5"), slot("d2"), 2048.0, A.mult)
        add(tt, slot("d6"), sv, slot("d3"), A.mult)
        add(tt, slot("d7"), ppv, slot("d4"), A.add)
        add(tt, slot("pin"), slot("d5"), pv, A.add)
        add(tt, slot("d8"), rv, slot("d6"), A.add)
        add(tt, slot("dz"), slot("d7"), pv, A.subtract)
        add(tt, slot("cn"), slot("d8"), nv, A.subtract)

    pv, sv = sub("ba0", 0), slot("side")
    for k in range(3):
        par, nxt = k % 2, 1 - k % 2
        last = k == 2
        q, qs, qk = T["q%d" % k], T["qs%d" % k], "q%d" % k
        dst = T.cores[(rank + STEP[k]) % N]
        la, lak = T["la%d" % k][:, 0:28], "la%d" % k
        ll, llk = T["lb%d" % par][:, 0:28], ["lb%d" % par, "lb0.l"][k == 0]
        lr, lrk = T["lb%d" % par][:, 32:60], ["lb%d" % par, "lb0.r"][k == 0]
        lak2 = "la%d" % (k + 1)
        la2 = T[lak2][:, 0:28]
        send(dst, "arq%d" % k, T["aq%d" % k][:, 0:C].bitcast(dt.uint8), q[:, 0:C].bitcast(dt.uint8), [qk])
        send(dst, "arq%d" % k, T["as%d" % k][:, 0:C], qs[:, 0:C], [qk])
        mm(0, T.uq[:], T.us[:], q[:, 0:H], qs[:, 0:H], ["uq", qk], H)
        mm(7, T.uq[:], T.us[:], q[:, H:C], qs[:, H:C], ["uq", qk], H)
        for b in range(4):
            mm(1 + b, blk("eq", b), blk("es", b), q[:], qs[:], ["eq%d" % b, qk])
        if k:
            derive(k, pv, sv, lv, rv)
            fill(3)
        op("v", lambda: V.tensor_copy(T.srow[:, 0:H], ps(0, H)), ["ps0"], ["srow.a"])
        op("s", lambda: S.activation(T.srow[:, H:C], ps(7, H), ACT.Copy), ["ps7"], ["srow.b"])
        sk = ["srow.a", "srow.b", "srow.n"]
        gather("s", row("sl"), T.srow[:, 0:456], sk, ll, llk)
        gather("s", row("sr"), T.srow[:, 0:456], sk, lr, lrk)
        if k:
            for i, w in ((1, lv), (2, rv)):
                op("s", lambda: S.activation(m3(i)[0], w[0], ACT.Identity, bias=T.c224[:, 4:5]), [w[1], "cm256"], [m3(i)[1]])
        else:
            gather("s", row("raa"), T.ra[:], ["ra", "ra.n"], lup, "lup")
            gather("s", row("pp"), T.prow[:], ["prow", "prow.n"], lup, "lup")
        for b in range(3):
            op("s", lambda: S.activation(T["fo%d" % b][:], ps(1 + b), ACT.Copy), ["ps%d" % (1 + b)], ["fo%d" % b])
        if k:
            fill(2)
        else:
            derive(k, pv, sv, lv, rv)
        gather("v", row("sa"), T.srow[:, 0:456], sk, la, lak)
        turn(T.sT[:], ["sT"], T.srow[:, 0:C], sk)
        turned("saT", "sa")
        s0, sav, slv, srv = plane("sT", 0), plane("saT", 0), plane("slT", 0), plane("srT", 0)
        turned("slT", "sl")
        tt(v3(0), sav, s0, A.subtract)
        turned("srT", "sr")
        tt(v3(1), s0, slv, A.subtract)
        tt(v3(2), s0, srv, A.subtract)
        tt(slot("m"), v3(0), v3(1), A.min)
        ts(slot("v0c"), v3(0), -1.0e-30, A.min)
        u0, u1 = sub("wu", 0), sub("wu", 1)
        tt(u0, slot("m"), v3(2), A.min)
        fill()
        for i in range(3):
            tt(slot("e%d" % i), v3(i), u0, A.is_equal)
        for i in range(3):
            tt(slot("t%d" % i), slot("e%d" % i), m3(i), A.mult)
        tt(slot("t3"), slot("t0"), slot("t1"), A.min)
        fill()
        tt(u1, slot("t3"), slot("t2"), A.min)
        fill()
        turn(T.urow[:, 0:C], ["urow"], T.wu[:], ["wu.0", "wu.1", "wu.i"])
        uk = ["urow", "urow.n"]
        gather("s", row("sl"), T.urow[:, 0:456], uk, ll, llk)
        fill()
        gather("v", row("sr"), T.urow[:, 0:456], uk, lr, lrk)
        if k == 0:
            late_constants()
        turned("ulT", "sl")
        turned("urT", "sr")
        tt(slot("m"), slot("v0c"), plane("ulT", 0), A.min)
        fill()
        m = tt(slot("mm"), slot("m"), plane("urT", 0), A.min)
        fill()
        tt(slot("e0"), v3(0), m, A.is_equal)
        tt(slot("e1"), plane("ulT", 0), m, A.is_equal)
        tt(slot("e2"), plane("urT", 0), m, A.is_equal)
        tt(slot("t0"), slot("e0"), m3(0), A.mult)
        tt(slot("t1"), slot("e1"), plane("ulT", 1), A.mult)
        tt(slot("t2"), slot("e2"), plane("urT", 1), A.mult)
        tt(slot("t3"), slot("t0"), slot("t1"), A.min)
        fill()
        tt(slot("t4"), slot("t2"), slot("t3"), A.min)
        fill()
        Q0 = ts(sub("wc_", 0), slot("t4"), 256.0, A.add)
        fill()
        turn(T.qrow[:, 0:C], ["qrow"], T.wc_[:], ["wc_.0", "wc_.i"])
        gather("s", row("qa"), T.qrow[:, 0:C], ["qrow"], la, lak)
        gather("s", row("qaa"), T.qa[:], ["qa"], la, lak)
        fill()
        gather("v", row("ql"), T.qrow[:], ["qrow", "qrow.n"], ll, llk)
        gather("s", row("qr"), T.qrow[:], ["qrow", "qrow.n"], lr, lrk)
        gather("s", row("qaaa"), T.qaa[:], ["qaa"], la, lak)
        fill(len(todo))
        turned("qaT", "qa")
        turned("qlT", "ql")
        Qa, Qaa, Qaaa, Ql, Qr = plane("qaT", 0), plane("qaaT", 0), plane("qaaaT", 0), plane("qlT", 0), plane("qrT", 0)
        eA = tt(slot("eA"), Q0, Qa, A.is_equal)
        xn = tt(slot("xn"), Qa, nv, A.is_equal)
        xl = tt(slot("xl"), Qa, lv, A.is_equal)
        xp = tt(slot("xp"), Qa, slot("pin"), A.is_equal)
        xr = tt(slot("xr"), Qa, rv, A.is_equal)
        eL = tt(slot("eL"), Ql, Qa, A.is_equal)
        rn = tt(slot("rn"), xn, eA, A.mult)
        yq = tt(slot("yq"), Qa, pv, A.subtract)
        yl = tt(slot("yl"), xl, eL, A.mult)
        turned("qaaT", "qaa")
        t = tt(slot("r0"), Qa, nv, A.subtract)
        eB = tt(slot("eB"), Qaa, Qa, A.is_equal)
        rot = tt(slot("rot"), rn, eB, A.mult)
        xb = tt(slot("xb"), xp, eB, A.mult)
        turned("qrT", "qr")
        rd = tt(slot("rd"), rot, slot("dz"), A.mult)
        eR = tt(slot("eR"), Qr, Qa, A.is_equal)
        xbd = tt(slot("xbd"), xb, slot("dz"), A.mult)
        yr = tt(slot("yr"), xr, eR, A.mult)
        rd = tt(slot("rd2"), rd, pv, A.add)
        yy = tt(slot("yy"), yl, yr, A.add)
        fr = tt(slot("r1"), rot, slot("cn"), A.mult)
        Y = tt(slot("Y"), yy, eA, A.mult)
        rs1 = tt(slot("rs1"), rot, sv, A.mult)
        yd = tt(slot("yd"), Y, yq, A.mult)
        turned("qaaaT", "qaaa")
        base = tt(slot("base"), rd, yd, A.add)
        eC = tt(slot("eC"), Qaaa, Qa, A.is_equal)
        t = tt(slot("r2"), Y, t, A.mult)
        cd = tt(slot("cd"), xbd, eC, A.mult)
        fr = tt(slot("r3"), fr, nv, A.add)
        pn = tt(sub("ba%d" % nxt, 0), base, cd, A.add)
        rs0 = tt(slot("rs0"), rot, rs1, A.subtract)
        turned_back("ba%d" % nxt, "rw", [0], lambda: tt(sub("wr", 0), fr, t, A.add))
        make_list(lak2, "ba%d" % nxt, [0])
        send(dst, "arl%d" % k, T["al%d" % k][:], la2, [lak2])
        wait("t", "arq%d" % k, 2 * len(topo.engines(core, dst)))
        fbank = [5, 6, 7, 0]
        for b in range(4):
            mm(fbank[b], blk("eq", b), blk("es", b), T["aq%d" % k][:], T["as%d" % k][:], ["eq%d" % b])
        for b in range(4):
            op("s", lambda: S.activation(T["fp%d" % b][:], ps(fbank[b]), ACT.Copy), ["ps%d" % fbank[b]], ["fp%d" % b])
            dma("y", "cf%d" % b, T.fq[:, C * b:C * b + C], T["fp%d" % b][:], ["fp%d" % b], ["fq%d" % b])
        turn(T.rrep[:, 0:C], ["rrep"], T.wr[:], ["wr.0", "wr.i"])
        rk = ["rrep", "rrep.n"]
        gather("s", row("repl"), T.rrep[:], rk, ll, llk)
        gather("v", row("repr_"), T.rrep[:], rk, lr, lrk)
        if not last:
            bl2 = sub("bl%d" % nxt, 2)
            op("s", lambda: S.activation(bl2[0], pn[0], ACT.Copy), [pn[1]], [bl2[1]])
        turned("replT", "repl")
        turned("reprT", "repr_")
        Rl, Rr = plane("replT", 0), plane("reprT", 0)
        lnew, rnew = sub("bl%d" % nxt, 0), sub("bl%d" % nxt, 1)
        t1 = tt(slot("l0"), pv, Rl, A.subtract)
        t2 = tt(slot("l1"), pv, Rr, A.subtract)
        t1 = tt(slot("l2"), rs1, t1, A.mult)
        t2 = tt(slot("l3"), rs0, t2, A.mult)
        tt(lnew, Rl, t1, A.add)
        tt(rnew, Rr, t2, A.add)
        if last:
            quantize(T.vq[:], T.vs[:], T.vt[:], ["vt"], ["vq"])
        wait("v", "arl%d" % k, len(topo.engines(core, dst)))
        wait("s", "arl%d" % k, len(topo.engines(core, dst)))
        al = T["al%d" % k]
        for b in range(4):
            fp, fq, kb = T["fp%d" % b], T.fq[:, C * b:C * b + C], T.kb[:, C * b:C * b + C]
            op("v", lambda: V.tensor_tensor(kb, fp[:].indirect(al[:]), fq, A.add), ["fp%d" % b, "fq%d" % b], ["kb%d" % b])
            if b < 3:
                op("s", lambda: S.activation(T.zt[:, b:4 * C:4], kb.indirect(al[:]), ACT.Copy, scale=0.5), ["kb%d" % b], ["zt%d" % b])
        op("s", lambda: S.activation(T.zt[:, 4 * H + 3:4 * C:4], kb.indirect(al[:, 14:28]), ACT.Copy, scale=0.5), ["kb3"], ["zt4"])
        op("v", lambda: V.tensor_scalar(T.zt[:, 3:4 * H:4], kb.indirect(al[:, 0:14]), 0.5, None, A.mult), ["kb3"], ["zt3"])
        quantize(T.zq[:], T.zs[:], T.zt[:], ["zt%d" % b for b in range(5)], ["zq"])
        mm(1, blk("wq", 0), blk("wp", 0), T.zq[:, 0:H], T.zs[:, 0:H], ["wq", "wp", "zq"], H)
        mm(5, blk("wq", 0), blk("wp", 0), T.zq[:, H:C], T.zs[:, H:C], ["wq", "wp", "zq"], H)
        wbank = [1, 2, 3, 6]
        for b in range(1, 4):
            mm(wbank[b], blk("wq", b), blk("wp", b), T.zq[:], T.zs[:], ["wq", "wp", "zq"])
        op("s", lambda: S.activation(T.rr0[:, 0:H], ps(1, H), ACT.Copy, scale=0.03125), ["ps1"], ["rr0.a"])
        op("s", lambda: S.activation(T.rr0[:, H:C], ps(5, H), ACT.Copy, scale=0.03125), ["ps5"], ["rr0.b"])
        for b in range(1, 4):
            op("s", lambda: S.activation(T["rr%d" % b][:], ps(wbank[b]), ACT.Copy, scale=0.03125), ["ps%d" % wbank[b]], ["rr%d" % b])
        gather("s", row("sa"), T.rr3[:], ["rr3"], la2, lak2)
        if not last:
            turned_back("bl%d" % nxt, "rw2", [0, 1, 2])
            make_list("lb%d" % nxt, "bl%d" % nxt, [0, 1])
            gather("s", row("pp"), T.rw2[:, 32:480], ["rw2"], la2, lak2)
            gather("s", row("raa"), T.pp[:], ["pp"], la2, lak2)
        else:
            e = tt(slot("f0"), pn, nv, A.is_equal)
            h = ts(slot("f1"), nv, -1.0, A.mult, 224.0, A.add)
            e = tt(slot("f2"), e, h, A.mult)
            tt(sub("bl1", 2), pn, e, A.add)
            turn(T.rp2[:], ["rp2"], T.bl1[:, 0:C], ["bl1.0", "bl1.1", "bl1.2", "bl1.i"])
            op("s", lambda: S.activation(T.trf[:], T.rp2[:], ACT.Identity, bias=T.c224[:, 0:1]), ["rp2", "c224"], ["trf"])
            for i in range(3):
                lane = (i + 2) % 3
                dma("y", "st_tr", T.tr[:, C * i:C * i + C], T.trf[lane:128:16, :], ["trf"], ["tr%d" % i])
        for b in range(3):
            rks = ["rr0.a", "rr0.b"] if b == 0 else ["rr%d" % b]
            op("v", lambda: V.tensor_tensor(T.xn[:, b:4 * C:4], T["rr%d" % b][:].indirect(la2), T["fo%d" % b][:], A.add),
               rks + ["fo%d" % b, lak2], ["xn%d" % b])
        tt((T.xn[:, 3:4 * C:4], "xn3"), row("sa"), (ps(4), "ps4"), A.add)
        quantize(T["q%d" % (k + 1)][:], T["qs%d" % (k + 1)][:], T.xn[:], ["xn%d" % b for b in range(4)], ["q%d" % (k + 1)])
        if not last:
            pv, lv, rv = pn, lnew, rnew

    mm(5, T.vq[:], T.vs[:], T.q3[:, 0:H], T.qs3[:, 0:H], ["vq", "q3"], H)
    mm(6, T.vq[:], T.vs[:], T.q3[:, H:C], T.qs3[:, H:C], ["vq", "q3"], H)
    dma("y", "st_oc", T.oc[:, 0:4 * C], T.q3[:, 0:C].bitcast(dt.uint8), ["q3"], ["oc"])
    for i in range(4):
        dma("y", "st_osc", T.osc[4 * i:4 * i + 4, :], T.qs3[32 * i:32 * i + 4, 0:C], ["q3"], ["osc%d" % i])
    op("v", lambda: V.tensor_copy(T.yt[:, 0:H], ps(5, H)), ["ps5"], ["yt.a"])
    op("s", lambda: S.activation(T.yt[:, H:C], ps(6, H), ACT.Copy), ["ps6"], ["yt.b"])
    dma("s", "st_y", T.y[:], T.yt[:], ["yt.a", "yt.b"], ["yo"])
    for sem in sorted(count):
        wait("g", sem, count[sem])
